import numpy as np
import ml_dtypes


def mxq(x, axis, fmt="e4m3"):
    dtype, down = {"e4m3": (ml_dtypes.float8_e4m3fn, 7), "e5m2": (ml_dtypes.float8_e5m2, 14)}[fmt]
    v = np.moveaxis(np.asarray(x, np.float32).astype(ml_dtypes.bfloat16).astype(np.float64), axis, -1)
    blocks = v.reshape(v.shape[:-1] + (-1, 32))
    amax = np.abs(blocks).max(-1, keepdims=True)
    byte = np.maximum(np.where(amax > 0, np.frexp(amax)[1] - 1 + 127, 0) - down, 1)
    scale = np.exp2(byte - 127.0)
    codes = (blocks / scale).astype(np.float32).astype(dtype).astype(np.float64)
    return np.moveaxis((codes * scale).reshape(v.shape), -1, axis)


WIDE = False


def mx_kscale(k):
    if not WIDE:
        return np.ones(k)
    levels = np.array([10, -10, 5, -5, 0])
    if k % 512:
        return np.exp2(np.random.permutation(np.resize(levels, k // 32))).repeat(32)
    a = np.empty((k // 512, 16))
    for p in range(k // 512):
        a[p, :8] = np.random.permutation(np.resize(levels, 8))
        for g in range(8):
            far = levels[np.abs(levels - a[p, g]) >= 10]
            a[p, g + 8] = far[np.random.randint(len(far))]
    return np.exp2(a.ravel()).repeat(32)


def f64(x):
    return np.asarray(x).astype(np.float64)


def striped(idx):
    return np.tile(idx.reshape(-1, 16).T, (8, 1)).astype(np.uint16)


def unstriped(offs):
    return offs[:16].T.reshape(-1).astype(np.int64)


def pack_weight(w):
    k, n = w.shape
    w = f64(np.asarray(w, np.float32).astype(ml_dtypes.bfloat16)).reshape(k // 32, 32, n)
    amax = np.abs(w).max(1)
    byte = np.clip(np.where(amax > 0, np.frexp(amax)[1] - 1 + 127 - 7, 1), 1, 254)
    scaled = (w * np.exp2(127.0 - byte)[:, None, :]).reshape(k, n).astype(np.float32)
    words = np.ascontiguousarray(scaled.reshape(k // 512, 128, 4, n).transpose(0, 1, 3, 2)).astype(ml_dtypes.float8_e4m3fn).view(np.uint8)
    return words, np.ascontiguousarray(byte.astype(np.uint8).reshape(k // 512, 16, n))


def unpack_weight(words, scales):
    g, p, n, _ = words.shape
    vals = np.ascontiguousarray(words).view(ml_dtypes.float8_e4m3fn).astype(np.float64) * np.repeat(np.exp2(scales.astype(np.float64) - 127.0), 8, axis=1)[..., None]
    return vals.transpose(0, 1, 3, 2).reshape(g * 512, n)


def relu(v):
    return np.maximum(v, 0.0)


K, T, H, N = 512, 1024, 512, 128


def setup_inputs():
    n = np.random.standard_normal
    s = mx_kscale(K)[:, None]
    u = mx_kscale(H)
    packed_xT = pack_weight(n((K, T)) * s)
    packed_w2 = pack_weight(n((H, N)) / np.sqrt(2 * H) / u[:, None])
    packed_w3 = pack_weight(n((H, N)) / np.sqrt(2 * H) / u[:, None])
    return {
        "x_words": packed_xT[0],
        "x_scales": packed_xT[1],
        "w1": (n((K, H)) / np.sqrt(K) / s * u).astype(np.float32),
        "w2_words": packed_w2[0],
        "w2_scales": packed_w2[1],
        "w3_words": packed_w3[0],
        "w3_scales": packed_w3[1],
        "pos1": striped(np.random.permutation(T)),
        "pos2": striped(np.random.permutation(T)),
    }


def reference(x_words, x_scales, w1, w2_words, w2_scales, w3_words, w3_scales, pos1, pos2):
    xq = unpack_weight(x_words, x_scales)
    h = relu(mxq(f64(w1), 0, "e4m3").T @ xq)
    z = np.maximum(h[:, unstriped(pos1)], h[:, unstriped(pos2)])
    return relu(unpack_weight(w2_words, w2_scales).T @ mxq(h, 0, "e4m3") + unpack_weight(w3_words, w3_scales).T @ mxq(z, 0, "e4m3"))

@@ -1,0 +1,215 @@
+from contextlib import ExitStack
+
+import concourse.mybir as mybir
+
+K, T, H, N = 512, 1024, 512, 128
+FLOPS = 2 * K * H * T + 2 * 2 * H * N * T
+
+F32 = mybir.dt.float32
+BF16 = mybir.dt.bfloat16
+I32 = mybir.dt.int32
+U32 = mybir.dt.uint32
+U16 = mybir.dt.uint16
+U8 = mybir.dt.uint8
+FP8X4 = mybir.dt.float8_e4m3fn_x4
+ACT = mybir.ActivationFunctionType
+ALU = mybir.AluOpType
+
+P = 128
+PACK = 4
+HALF = 512
+QUARTER = 256
+WIDE = 1376
+RUN = 64
+CHUNKS = (256, 256, 256, 128, 128)
+
+
+def tile_picked_wsagecat_maxrelu_l_kernel(
+    tc, x_words, x_scales, w1, w2_words, w2_scales, w3_words, w3_scales, pos1, pos2, out
+):
+    nc = tc.nc
+    with ExitStack() as ctx:
+        keep = ctx.enter_context(tc.tile_pool(name="keep", bufs=1))
+        psum = ctx.enter_context(tc.psum_pool(name="psum", bufs=1))
+
+        def load_scales(tile, cols, src):
+            for q in range(4):
+                nc.sync.dma_start(
+                    out=tile[32 * q : 32 * q + 4, cols].bitcast(I32),
+                    in_=src[0, 4 * q : 4 * q + 4, :].bitcast(I32),
+                )
+
+        def load_words(tile, src):
+            nc.sync.dma_start(out=tile.bitcast(I32), in_=src[0].rearrange("p n t -> p (n t)").bitcast(I32))
+
+        x_sc = keep.tile([P, QUARTER], U8, name="x_sc", align_bytes=64)
+        nc.vector.memset(x_sc[:].bitcast(U32), 0)
+        w1_raw = keep.tile([P, PACK, H], F32, name="w1_raw", tag="w1_raw", align_bytes=64)
+        nc.sync.dma_start(out=w1_raw[:], in_=w1.rearrange("(p j) c -> p j c", j=PACK))
+        for q in range(4):
+            queue = nc.gpsimd if q == 3 else nc.scalar
+            queue.dma_start(
+                out=x_sc[32 * q : 32 * q + 16, :].bitcast(I32),
+                in_=x_scales[0, 4 * q : 4 * q + 4, :].bitcast(I32).rearrange("r (a c) -> a r c", a=4),
+            )
+        x_w = keep.tile([P, T], U32, name="x_w", align_bytes=64)
+        x_src = x_words[0].rearrange("p n t -> p (n t)").bitcast(I32)
+        for c0 in (0, HALF):
+            nc.sync.dma_start(out=x_w[:, c0 : c0 + HALF].bitcast(I32), in_=x_src[:, c0 : c0 + HALF])
+        lists = []
+        for name, src in (("pos1_sb", pos1), ("pos2_sb", pos2)):
+            tile = keep.tile([P, T // 16], U16, name=name)
+            nc.sync.dma_start(tile[:], src)
+            lists.append(tile)
+
+        w1_b = keep.tile([P, PACK, P, PACK], BF16, name="w1_b", tag="w1_b", align_bytes=64)
+        w1_q = keep.tile([P, H], U32, name="w1_q", align_bytes=64)
+        w1_sc = keep.tile([P, H], U8, name="w1_sc", align_bytes=64)
+        w1_src = w1_raw[:].rearrange("p j (m t) -> p m t j", t=PACK)
+        w1_dst = w1_b[:].rearrange("p t m j -> p m t j")
+
+        def quant_w1(t0, t1):
+            nc.vector.quantize_mx(
+                out=w1_q[:, t0 * P : t1 * P].bitcast(FP8X4),
+                scales=w1_sc[:, t0 * P : t1 * P],
+                in_=w1_b[:, t0:t1, :, :].rearrange("p t m j -> p (t m j)"),
+            )
+
+        nc.vector.tensor_copy(out=w1_dst[:, :, 0, :], in_=w1_src[:, :, 0, :])
+        nc.scalar.activation(out=w1_dst[:, :, 2:4, :], in_=w1_src[:, :, 2:4, :], func=ACT.Copy)
+        quant_w1(0, 1)
+        nc.vector.tensor_copy(out=w1_dst[:, :, 1, :], in_=w1_src[:, :, 1, :])
+        quant_w1(1, 2)
+
+        h = keep.tile([P, PACK * T], F32, name="h", align_bytes=64)
+
+        def first_layer(t):
+            width = QUARTER if t == 0 else HALF
+            for c0 in range(0, T, width):
+                acc = psum.tile([P, HALF], F32, name="acc", tag="acc", bufs=8)
+                for a in range(c0 // QUARTER, (c0 + width) // QUARTER):
+                    cols = slice(a * QUARTER, (a + 1) * QUARTER)
+                    nc.tensor.matmul_mx(
+                        out=acc[:, a * QUARTER - c0 : (a + 1) * QUARTER - c0],
+                        lhsT=w1_q[:, t * P : (t + 1) * P].bitcast(FP8X4),
+                        lhsT_scale=w1_sc[:, t * P : (t + 1) * P],
+                        rhs=x_w[:, cols].bitcast(FP8X4),
+                        rhs_scale=x_sc[4 * a :, :],
+                        start=True,
+                        stop=True,
+                    )
+                dst = h[:, t * T + c0 : t * T + c0 + width]
+                if t == 0 and c0 % HALF == QUARTER:
+                    nc.vector.tensor_scalar_max(out=dst, in0=acc[:, :width], scalar1=0.0)
+                else:
+                    nc.scalar.activation(out=dst, in_=acc[:, :width], func=ACT.Relu)
+
+        first_layer(0)
+        quant_w1(2, 4)
+        for t in range(1, PACK):
+            first_layer(t)
+
+        w23 = keep.tile([P, 2 * N], U32, name="w23", tag="w1_raw", align_bytes=64)
+        w23_sc = keep.tile([P, 2 * N], U8, name="w23_sc", tag="w1_b", align_bytes=64)
+        nc.gpsimd.memset(w23_sc[:].bitcast(U32), 0)
+        load_words(w23[:, 0:N], w2_words)
+        load_words(w23[:, N : 2 * N], w3_words)
+        load_scales(w23_sc, slice(0, N), w2_scales)
+        load_scales(w23_sc, slice(N, 2 * N), w3_scales)
+
+        h_b = keep.tile([P, T, PACK], BF16, name="h_b", align_bytes=64)
+        h_q = keep.tile([P, T], U32, name="h_q", align_bytes=64)
+        h_sc = keep.tile([P, T], U8, name="h_sc", align_bytes=64)
+        h_src = h[:].rearrange("p (t c i) -> p c t i", t=PACK, i=4)
+        h_dst = h_b[:].rearrange("p (c i) t -> p c t i", i=4)
+        for half in range(2):
+            groups = slice(half * HALF // 4, (half + 1) * HALF // 4)
+            nc.scalar.copy(out=h_dst[:, groups, :, :], in_=h_src[:, groups, :, :])
+
+        def quantize(codes, scales, values, c0, c1):
+            nc.vector.quantize_mx(
+                out=codes[:, c0:c1].bitcast(FP8X4),
+                scales=scales[:, c0:c1],
+                in_=values[:, c0:c1, :].rearrange("p c t -> p (c t)"),
+            )
+
+        picked = [keep.tile([P, T // RUN, PACK, RUN], BF16, name=f"picked{d}", align_bytes=64) for d in range(2)]
+        z = keep.tile([P, T // RUN, PACK, RUN], BF16, name="z", align_bytes=64)
+        z_b = keep.tile([P, T, PACK], BF16, name="z_b", align_bytes=64)
+        z_q = keep.tile([P, T], U32, name="z_q", align_bytes=64)
+        z_sc = keep.tile([P, T], U8, name="z_sc", align_bytes=64)
+        res = keep.tile([P, T], F32, name="res", align_bytes=64)
+
+        def gather(d, t, c0, c1):
+            nc.vector.tensor_copy(
+                out=picked[d][:, c0 // RUN : c1 // RUN, t, :],
+                in_=h[:, t * T : t * T + (WIDE if c1 - c0 == T else T)].indirect(lists[d][:, c0 // 16 : c1 // 16]),
+            )
+
+        def largest(t, c0, c1):
+            runs = slice(c0 // RUN, c1 // RUN)
+            nc.vector.tensor_tensor(
+                out=z[:, runs, t, :], in0=picked[0][:, runs, t, :], in1=picked[1][:, runs, t, :], op=ALU.max
+            )
+
+        def interleave(c0, c1):
+            nc.scalar.copy(
+                out=z_b[:, c0:c1, :].rearrange("p (b c i) t -> p b c t i", c=RUN // 4, i=4),
+                in_=z[:, c0 // RUN : c1 // RUN, :, :].rearrange("p b t (c i) -> p b c t i", i=4),
+            )
+
+        accs = {}
+
+        def own_pass(c0, c1):
+            accs[c0] = psum.tile([P, HALF], F32, name="acc", tag="acc", bufs=8)
+            nc.tensor.matmul_mx(
+                out=accs[c0][:, : c1 - c0],
+                lhsT=w23[:, 0:N].bitcast(FP8X4),
+                lhsT_scale=w23_sc[:, 0:N],
+                rhs=h_q[:, c0:c1].bitcast(FP8X4),
+                rhs_scale=h_sc[:, c0:c1],
+                start=True,
+                stop=False,
+            )
+
+        def finish(c0, c1):
+            quantize(z_q, z_sc, z_b, c0, c1)
+            nc.tensor.matmul_mx(
+                out=accs[c0][:, : c1 - c0],
+                lhsT=w23[:, N : 2 * N].bitcast(FP8X4),
+                lhsT_scale=w23_sc[:, N : 2 * N],
+                rhs=z_q[:, c0:c1].bitcast(FP8X4),
+                rhs_scale=z_sc[:, c0:c1],
+                start=False,
+                stop=True,
+            )
+            nc.scalar.activation(out=res[:, c0:c1], in_=accs[c0][:, : c1 - c0], func=ACT.Relu)
+            nc.sync.dma_start(out=out[:, c0:c1], in_=res[:, c0:c1])
+
+        edges = [sum(CHUNKS[:n]) for n in range(len(CHUNKS) + 1)]
+        spans = list(zip(edges[:-1], edges[1:]))
+        gather(0, 0, 0, HALF)
+        gather(0, 0, HALF, T)
+        gather(1, 0, 0, HALF)
+        gather(1, 0, HALF, T)
+        for t in (1, 2):
+            gather(0, t, 0, T)
+            largest(t - 1, 0, T)
+            gather(1, t, 0, T)
+        for n, span in enumerate(spans):
+            gather(0, PACK - 1, *span)
+            if n == 0:
+                largest(PACK - 2, 0, T)
+            elif n < len(spans) - 1:
+                largest(PACK - 1, *spans[n - 1])
+            gather(1, PACK - 1, *span)
+        for span in spans[-2:]:
+            largest(PACK - 1, *span)
+        for span in spans:
+            interleave(*span)
+        for c0 in (0, HALF):
+            quantize(h_q, h_sc, h_b, c0, c0 + HALF)
+        for span in spans:
+            own_pass(*span)
+        for span in spans:
+            finish(*span)

@@ -19,9 +19,8 @@ P = 128
 PACK = 4
 HALF = 512
 QUARTER = 256
-WIDE = 1376
 RUN = 64
-CHUNKS = (256, 256, 256, 128, 128)
+CHUNKS = (512, 256, 128, 128)
 
 
 def tile_picked_wsagecat_maxrelu_l_kernel(
@@ -44,11 +43,13 @@ def tile_picked_wsagecat_maxrelu_l_kernel(
 
         x_sc = keep.tile([P, QUARTER], U8, name="x_sc", align_bytes=64)
         nc.vector.memset(x_sc[:].bitcast(U32), 0)
-        w1_raw = keep.tile([P, PACK, H], F32, name="w1_raw", tag="w1_raw", align_bytes=64)
-        nc.sync.dma_start(out=w1_raw[:], in_=w1.rearrange("(p j) c -> p j c", j=PACK))
+        w1_raw = keep.tile([P, PACK, H // 2], F32, name="w1_raw", tag="w1_raw", align_bytes=64)
+        w1_hi = keep.tile([P, PACK, H // 2], F32, name="w1_hi", align_bytes=64)
+        w1_rows = w1.rearrange("(p j) c -> p j c", j=PACK)
+        nc.sync.dma_start(out=w1_raw[:], in_=w1_rows[:, :, : H // 2])
+        nc.sync.dma_start(out=w1_hi[:], in_=w1_rows[:, :, H // 2 :])
         for q in range(4):
-            queue = nc.gpsimd if q == 3 else nc.scalar
-            queue.dma_start(
+            nc.sync.dma_start(
                 out=x_sc[32 * q : 32 * q + 16, :].bitcast(I32),
                 in_=x_scales[0, 4 * q : 4 * q + 4, :].bitcast(I32).rearrange("r (a c) -> a r c", a=4),
             )
@@ -65,7 +66,8 @@ def tile_picked_wsagecat_maxrelu_l_kernel(
         w1_b = keep.tile([P, PACK, P, PACK], BF16, name="w1_b", tag="w1_b", align_bytes=64)
         w1_q = keep.tile([P, H], U32, name="w1_q", align_bytes=64)
         w1_sc = keep.tile([P, H], U8, name="w1_sc", align_bytes=64)
-        w1_src = w1_raw[:].rearrange("p j (m t) -> p m t j", t=PACK)
+        lo_src = w1_raw[:].rearrange("p j (m t) -> p m t j", t=PACK)
+        hi_src = w1_hi[:].rearrange("p j (m t) -> p m t j", t=PACK)
         w1_dst = w1_b[:].rearrange("p t m j -> p m t j")
 
         def quant_w1(t0, t1):
@@ -75,18 +77,22 @@ def tile_picked_wsagecat_maxrelu_l_kernel(
                 in_=w1_b[:, t0:t1, :, :].rearrange("p t m j -> p (t m j)"),
             )
 
-        nc.vector.tensor_copy(out=w1_dst[:, :, 0, :], in_=w1_src[:, :, 0, :])
-        nc.scalar.activation(out=w1_dst[:, :, 2:4, :], in_=w1_src[:, :, 2:4, :], func=ACT.Copy)
+        nc.vector.tensor_copy(out=w1_dst[:, : P // 2, :, :], in_=lo_src)
+        nc.vector.tensor_copy(out=w1_dst[:, P // 2 :, 0, :], in_=hi_src[:, :, 0, :])
+        nc.scalar.activation(out=w1_dst[:, P // 2 :, 1:4, :], in_=hi_src[:, :, 1:4, :], func=ACT.Copy)
         quant_w1(0, 1)
-        nc.vector.tensor_copy(out=w1_dst[:, :, 1, :], in_=w1_src[:, :, 1, :])
         quant_w1(1, 2)
+        quant_w1(2, 4)
 
         h = keep.tile([P, PACK * T], F32, name="h", align_bytes=64)
+
+        filled = []
 
         def first_layer(t):
             width = QUARTER if t == 0 else HALF
             for c0 in range(0, T, width):
-                acc = psum.tile([P, HALF], F32, name="acc", tag="acc", bufs=8)
+                acc = psum.tile([P, HALF], F32, name="h_acc", tag=f"h_acc{len(filled) % 4}")
+                filled.append(acc)
                 for a in range(c0 // QUARTER, (c0 + width) // QUARTER):
                     cols = slice(a * QUARTER, (a + 1) * QUARTER)
                     nc.tensor.matmul_mx(
@@ -99,14 +105,12 @@ def tile_picked_wsagecat_maxrelu_l_kernel(
                         stop=True,
                     )
                 dst = h[:, t * T + c0 : t * T + c0 + width]
-                if t == 0 and c0 % HALF == QUARTER:
+                if t == 0 and c0 % HALF == 0:
                     nc.vector.tensor_scalar_max(out=dst, in0=acc[:, :width], scalar1=0.0)
                 else:
                     nc.scalar.activation(out=dst, in_=acc[:, :width], func=ACT.Relu)
 
-        first_layer(0)
-        quant_w1(2, 4)
-        for t in range(1, PACK):
+        for t in range(PACK):
             first_layer(t)
 
         w23 = keep.tile([P, 2 * N], U32, name="w23", tag="w1_raw", align_bytes=64)
@@ -143,13 +147,16 @@ def tile_picked_wsagecat_maxrelu_l_kernel(
         def gather(d, t, c0, c1):
             nc.vector.tensor_copy(
                 out=picked[d][:, c0 // RUN : c1 // RUN, t, :],
-                in_=h[:, t * T : t * T + (WIDE if c1 - c0 == T else T)].indirect(lists[d][:, c0 // 16 : c1 // 16]),
+                in_=h[:, t * T : (t + 1) * T].indirect(lists[d][:, c0 // 16 : c1 // 16]),
             )
 
-        def largest(t, c0, c1):
+        def largest(t0, t1, c0, c1):
             runs = slice(c0 // RUN, c1 // RUN)
             nc.vector.tensor_tensor(
-                out=z[:, runs, t, :], in0=picked[0][:, runs, t, :], in1=picked[1][:, runs, t, :], op=ALU.max
+                out=z[:, runs, t0:t1, :],
+                in0=picked[0][:, runs, t0:t1, :],
+                in1=picked[1][:, runs, t0:t1, :],
+                op=ALU.max,
             )
 
         def interleave(c0, c1):
@@ -161,7 +168,7 @@ def tile_picked_wsagecat_maxrelu_l_kernel(
         accs = {}
 
         def own_pass(c0, c1):
-            accs[c0] = psum.tile([P, HALF], F32, name="acc", tag="acc", bufs=8)
+            accs[c0] = psum.tile([P, HALF], F32, name=f"out_acc{c0}")
             nc.tensor.matmul_mx(
                 out=accs[c0][:, : c1 - c0],
                 lhsT=w23[:, 0:N].bitcast(FP8X4),
@@ -183,28 +190,40 @@ def tile_picked_wsagecat_maxrelu_l_kernel(
                 start=False,
                 stop=True,
             )
-            nc.scalar.activation(out=res[:, c0:c1], in_=accs[c0][:, : c1 - c0], func=ACT.Relu)
+
+        def store(c0, c1):
+            if c1 - c0 > P:
+                nc.scalar.activation(out=res[:, c0:c1], in_=accs[c0][:, : c1 - c0], func=ACT.Relu)
+            else:
+                nc.vector.tensor_scalar_max(out=res[:, c0:c1], in0=accs[c0][:, : c1 - c0], scalar1=0.0)
             nc.sync.dma_start(out=out[:, c0:c1], in_=res[:, c0:c1])
 
         edges = [sum(CHUNKS[:n]) for n in range(len(CHUNKS) + 1)]
         spans = list(zip(edges[:-1], edges[1:]))
-        gather(0, 0, 0, HALF)
-        gather(0, 0, HALF, T)
-        gather(1, 0, 0, HALF)
-        gather(1, 0, HALF, T)
-        for t in (1, 2):
-            gather(0, t, 0, T)
-            largest(t - 1, 0, T)
-            gather(1, t, 0, T)
-        for n, span in enumerate(spans):
-            gather(0, PACK - 1, *span)
-            if n == 0:
-                largest(PACK - 2, 0, T)
-            elif n < len(spans) - 1:
-                largest(PACK - 1, *spans[n - 1])
-            gather(1, PACK - 1, *span)
-        for span in spans[-2:]:
-            largest(PACK - 1, *span)
+        for t in (0, 1):
+            for d in range(2):
+                for c0 in (0, HALF):
+                    gather(d, t, c0, c0 + HALF)
+                    if (t, d, c0) == (1, 0, 0):
+                        largest(0, 1, 0, T)
+        gather(0, 2, 0, HALF)
+        largest(1, 2, 0, T)
+        gather(1, 2, 0, HALF)
+        gather(0, 3, 0, HALF)
+        gather(1, 3, 0, HALF)
+        gather(0, 2, HALF, T)
+        largest(2, 4, 0, HALF)
+        gather(1, 2, HALF, T)
+        gather(0, 3, *spans[1])
+        largest(2, 3, HALF, T)
+        gather(1, 3, *spans[1])
+        gather(0, 3, *spans[2])
+        largest(3, 4, *spans[1])
+        gather(1, 3, *spans[2])
+        gather(0, 3, *spans[3])
+        gather(1, 3, *spans[3])
+        largest(3, 4, *spans[2])
+        largest(3, 4, *spans[3])
         for span in spans:
             interleave(*span)
         for c0 in (0, HALF):
@@ -213,3 +232,5 @@ def tile_picked_wsagecat_maxrelu_l_kernel(
             own_pass(*span)
         for span in spans:
             finish(*span)
+        for span in spans:
+            store(*span)

@@ -20,7 +20,7 @@ PACK = 4
 HALF = 512
 QUARTER = 256
 RUN = 64
-CHUNKS = (512, 256, 128, 128)
+CHUNKS = (256, 256, 256, 128, 128)
 
 
 def tile_picked_wsagecat_maxrelu_l_kernel(
@@ -91,7 +91,7 @@ def tile_picked_wsagecat_maxrelu_l_kernel(
         def first_layer(t):
             width = QUARTER if t == 0 else HALF
             for c0 in range(0, T, width):
-                acc = psum.tile([P, HALF], F32, name="h_acc", tag=f"h_acc{len(filled) % 4}")
+                acc = psum.tile([P, HALF], F32, name="h_acc", tag=f"bank{len(filled) % 4}")
                 filled.append(acc)
                 for a in range(c0 // QUARTER, (c0 + width) // QUARTER):
                     cols = slice(a * QUARTER, (a + 1) * QUARTER)
@@ -121,13 +121,15 @@ def tile_picked_wsagecat_maxrelu_l_kernel(
         load_scales(w23_sc, slice(0, N), w2_scales)
         load_scales(w23_sc, slice(N, 2 * N), w3_scales)
 
-        h_b = keep.tile([P, T, PACK], BF16, name="h_b", align_bytes=64)
+        h_flat = keep.tile([P, T * PACK], BF16, name="h_flat", align_bytes=64)
+        h_b = h_flat[:].rearrange("p (c t) -> p c t", t=PACK)
         h_q = keep.tile([P, T], U32, name="h_q", align_bytes=64)
         h_sc = keep.tile([P, T], U8, name="h_sc", align_bytes=64)
         h_src = h[:].rearrange("p (t c i) -> p c t i", t=PACK, i=4)
-        h_dst = h_b[:].rearrange("p (c i) t -> p c t i", i=4)
-        for half in range(2):
-            groups = slice(half * HALF // 4, (half + 1) * HALF // 4)
+        h_dst = h_b.rearrange("p (c i) t -> p c t i", i=4)
+
+        def interleave_h(a):
+            groups = slice(a * QUARTER // 4, (a + 1) * QUARTER // 4)
             nc.scalar.copy(out=h_dst[:, groups, :, :], in_=h_src[:, groups, :, :])
 
         def quantize(codes, scales, values, c0, c1):
@@ -138,7 +140,7 @@ def tile_picked_wsagecat_maxrelu_l_kernel(
             )
 
         picked = [keep.tile([P, T // RUN, PACK, RUN], BF16, name=f"picked{d}", align_bytes=64) for d in range(2)]
-        z = keep.tile([P, T // RUN, PACK, RUN], BF16, name="z", align_bytes=64)
+        z = keep.tile([P, PACK, T], BF16, name="z", align_bytes=64)
         z_b = keep.tile([P, T, PACK], BF16, name="z_b", align_bytes=64)
         z_q = keep.tile([P, T], U32, name="z_q", align_bytes=64)
         z_sc = keep.tile([P, T], U8, name="z_sc", align_bytes=64)
@@ -153,7 +155,7 @@ def tile_picked_wsagecat_maxrelu_l_kernel(
         def largest(t0, t1, c0, c1):
             runs = slice(c0 // RUN, c1 // RUN)
             nc.vector.tensor_tensor(
-                out=z[:, runs, t0:t1, :],
+                out=z[:, t0:t1, c0:c1].rearrange("p t (b r) -> p b t r", r=RUN),
                 in0=picked[0][:, runs, t0:t1, :],
                 in1=picked[1][:, runs, t0:t1, :],
                 op=ALU.max,
@@ -161,14 +163,14 @@ def tile_picked_wsagecat_maxrelu_l_kernel(
 
         def interleave(c0, c1):
             nc.scalar.copy(
-                out=z_b[:, c0:c1, :].rearrange("p (b c i) t -> p b c t i", c=RUN // 4, i=4),
-                in_=z[:, c0 // RUN : c1 // RUN, :, :].rearrange("p b t (c i) -> p b c t i", i=4),
+                out=z_b[:, c0:c1, :].rearrange("p (c i) t -> p c t i", i=4),
+                in_=z[:, :, c0:c1].rearrange("p t (c i) -> p c t i", i=4),
             )
 
         accs = {}
 
         def own_pass(c0, c1):
-            accs[c0] = psum.tile([P, HALF], F32, name=f"out_acc{c0}")
+            accs[c0] = psum.tile([P, HALF], F32, name="out_acc", tag=f"bank{(4 + len(accs)) % 8}")
             nc.tensor.matmul_mx(
                 out=accs[c0][:, : c1 - c0],
                 lhsT=w23[:, 0:N].bitcast(FP8X4),
@@ -200,30 +202,53 @@ def tile_picked_wsagecat_maxrelu_l_kernel(
 
         edges = [sum(CHUNKS[:n]) for n in range(len(CHUNKS) + 1)]
         spans = list(zip(edges[:-1], edges[1:]))
-        for t in (0, 1):
+        diff = keep.tile([P, 2, 2, QUARTER], F32, name="diff", align_bytes=64)
+        units = [(0, 0), (0, HALF), (1, HALF), (1, 0)]
+        pairs = []
+
+        def add_back(u):
+            t, c0 = units[u]
+            nc.gpsimd.tensor_tensor(
+                out=z[:, t, c0 : c0 + HALF].rearrange("p (b r) -> p b r", b=2),
+                in0=diff[:, u % 2, :, :],
+                in1=pairs[u][:, :, 1, :],
+                op=ALU.add,
+            )
+
+        for u, (t, c0) in enumerate(units):
+            pair = h_flat[:, u * T : (u + 1) * T].rearrange("p (b d r) -> p b d r", b=2, d=2)
+            pairs.append(pair)
             for d in range(2):
-                for c0 in (0, HALF):
-                    gather(d, t, c0, c0 + HALF)
-                    if (t, d, c0) == (1, 0, 0):
-                        largest(0, 1, 0, T)
+                nc.vector.tensor_copy(
+                    out=pair[:, :, d, :],
+                    in_=h[:, t * T : (t + 1) * T].indirect(lists[d][:, c0 // 16 : (c0 + HALF) // 16]),
+                )
+            nc.gpsimd.tensor_tensor(
+                out=diff[:, u % 2, :, :], in0=pair[:, :, 0, :], in1=pair[:, :, 1, :], op=ALU.subtract
+            )
+            nc.scalar.activation(out=diff[:, u % 2, :, :], in_=diff[:, u % 2, :, :], func=ACT.Relu)
+            if u > 0:
+                add_back(u - 1)
+        add_back(len(units) - 1)
+        for a in range(4):
+            interleave_h(a)
         gather(0, 2, 0, HALF)
-        largest(1, 2, 0, T)
         gather(1, 2, 0, HALF)
         gather(0, 3, 0, HALF)
         gather(1, 3, 0, HALF)
         gather(0, 2, HALF, T)
         largest(2, 4, 0, HALF)
         gather(1, 2, HALF, T)
-        gather(0, 3, *spans[1])
-        largest(2, 3, HALF, T)
-        gather(1, 3, *spans[1])
         gather(0, 3, *spans[2])
-        largest(3, 4, *spans[1])
+        largest(2, 3, HALF, T)
         gather(1, 3, *spans[2])
         gather(0, 3, *spans[3])
-        gather(1, 3, *spans[3])
         largest(3, 4, *spans[2])
+        gather(1, 3, *spans[3])
+        gather(0, 3, *spans[4])
+        gather(1, 3, *spans[4])
         largest(3, 4, *spans[3])
+        largest(3, 4, *spans[4])
         for span in spans:
             interleave(*span)
         for c0 in (0, HALF):

@@ -237,18 +237,16 @@ def tile_picked_wsagecat_maxrelu_l_kernel(
         gather(0, 3, 0, HALF)
         gather(1, 3, 0, HALF)
         gather(0, 2, HALF, T)
-        largest(2, 4, 0, HALF)
         gather(1, 2, HALF, T)
+        largest(2, 4, 0, HALF)
         gather(0, 3, *spans[2])
-        largest(2, 3, HALF, T)
         gather(1, 3, *spans[2])
-        gather(0, 3, *spans[3])
-        largest(3, 4, *spans[2])
+        gather(0, 3, spans[3][0], T)
+        largest(2, 4, *spans[2])
         gather(1, 3, *spans[3])
-        gather(0, 3, *spans[4])
         gather(1, 3, *spans[4])
-        largest(3, 4, *spans[3])
-        largest(3, 4, *spans[4])
+        largest(2, 4, *spans[3])
+        largest(2, 4, *spans[4])
         for span in spans:
             interleave(*span)
         for c0 in (0, HALF):

@@ -19,6 +19,7 @@ P = 128
 PACK = 4
 HALF = 512
 QUARTER = 256
+WIDE = 1376
 RUN = 64
 CHUNKS = (256, 256, 256, 128, 128)
 
@@ -149,7 +150,7 @@ def tile_picked_wsagecat_maxrelu_l_kernel(
         def gather(d, t, c0, c1):
             nc.vector.tensor_copy(
                 out=picked[d][:, c0 // RUN : c1 // RUN, t, :],
-                in_=h[:, t * T : (t + 1) * T].indirect(lists[d][:, c0 // 16 : c1 // 16]),
+                in_=h[:, t * T : t * T + (WIDE if c1 - c0 == T else T)].indirect(lists[d][:, c0 // 16 : c1 // 16]),
             )
 
         def largest(t0, t1, c0, c1):
@@ -232,25 +233,21 @@ def tile_picked_wsagecat_maxrelu_l_kernel(
         add_back(len(units) - 1)
         for a in range(4):
             interleave_h(a)
-        gather(0, 2, 0, HALF)
+        gather(0, 2, 0, T)
         gather(1, 2, 0, HALF)
         gather(0, 3, 0, HALF)
         gather(1, 3, 0, HALF)
-        gather(0, 2, HALF, T)
         gather(1, 2, HALF, T)
         largest(2, 4, 0, HALF)
-        gather(0, 3, *spans[2])
-        gather(1, 3, *spans[2])
-        gather(0, 3, spans[3][0], T)
-        largest(2, 4, *spans[2])
-        gather(1, 3, *spans[3])
-        gather(1, 3, *spans[4])
-        largest(2, 4, *spans[3])
-        largest(2, 4, *spans[4])
+        gather(0, 3, HALF, T)
+        gather(1, 3, HALF, HALF + QUARTER)
+        gather(1, 3, HALF + QUARTER, T)
+        largest(2, 4, HALF, HALF + QUARTER)
+        largest(2, 4, HALF + QUARTER, T)
         for span in spans:
             interleave(*span)
-        for c0 in (0, HALF):
-            quantize(h_q, h_sc, h_b, c0, c0 + HALF)
+        for c0 in range(0, T, QUARTER):
+            quantize(h_q, h_sc, h_b, c0, c0 + QUARTER)
         for span in spans:
             own_pass(*span)
         for span in spans:

@@ -19,7 +19,6 @@ P = 128
 PACK = 4
 HALF = 512
 QUARTER = 256
-WIDE = 1376
 RUN = 64
 CHUNKS = (256, 256, 256, 128, 128)
 
@@ -122,77 +121,75 @@ def tile_picked_wsagecat_maxrelu_l_kernel(
         load_scales(w23_sc, slice(0, N), w2_scales)
         load_scales(w23_sc, slice(N, 2 * N), w3_scales)
 
-        h_flat = keep.tile([P, T * PACK], BF16, name="h_flat", align_bytes=64)
-        h_b = h_flat[:].rearrange("p (c t) -> p c t", t=PACK)
-        h_q = keep.tile([P, T], U32, name="h_q", align_bytes=64)
+        h_b = []
         h_sc = keep.tile([P, T], U8, name="h_sc", align_bytes=64)
         h_src = h[:].rearrange("p (t c i) -> p c t i", t=PACK, i=4)
-        h_dst = h_b.rearrange("p (c i) t -> p c t i", i=4)
 
-        def interleave_h(a):
+        def interleave_h(a, room):
             groups = slice(a * QUARTER // 4, (a + 1) * QUARTER // 4)
-            nc.scalar.copy(out=h_dst[:, groups, :, :], in_=h_src[:, groups, :, :])
+            tile = keep.tile([P, QUARTER, PACK], BF16, name=f"h_b{a}", tag=room, align_bytes=64)
+            h_b.append(tile)
+            nc.scalar.copy(out=tile[:].rearrange("p (c i) t -> p c t i", i=4), in_=h_src[:, groups, :, :])
 
         def quantize(codes, scales, values, c0, c1):
             nc.vector.quantize_mx(
                 out=codes[:, c0:c1].bitcast(FP8X4),
                 scales=scales[:, c0:c1],
-                in_=values[:, c0:c1, :].rearrange("p c t -> p (c t)"),
+                in_=values.rearrange("p c t -> p (c t)"),
             )
 
-        picked = [keep.tile([P, T // RUN, PACK, RUN], BF16, name=f"picked{d}", align_bytes=64) for d in range(2)]
-        z = keep.tile([P, PACK, T], BF16, name="z", align_bytes=64)
+        picked = []
+        z = [keep.tile([P, PACK, HALF], BF16, name=f"z{n}", tag=f"z{n}", align_bytes=64) for n in range(2)]
         z_b = keep.tile([P, T, PACK], BF16, name="z_b", align_bytes=64)
-        z_q = keep.tile([P, T], U32, name="z_q", align_bytes=64)
         z_sc = keep.tile([P, T], U8, name="z_sc", align_bytes=64)
-        res = keep.tile([P, T], F32, name="res", align_bytes=64)
 
         def gather(d, t, c0, c1):
             nc.vector.tensor_copy(
-                out=picked[d][:, c0 // RUN : c1 // RUN, t, :],
-                in_=h[:, t * T : t * T + (WIDE if c1 - c0 == T else T)].indirect(lists[d][:, c0 // 16 : c1 // 16]),
+                out=picked[d][:, (c0 - HALF) // RUN : (c1 - HALF) // RUN, t - 2, :],
+                in_=h[:, t * T : (t + 1) * T].indirect(lists[d][:, c0 // 16 : c1 // 16]),
             )
 
         def largest(t0, t1, c0, c1):
-            runs = slice(c0 // RUN, c1 // RUN)
+            runs = slice((c0 - HALF) // RUN, (c1 - HALF) // RUN)
             nc.vector.tensor_tensor(
-                out=z[:, t0:t1, c0:c1].rearrange("p t (b r) -> p b t r", r=RUN),
-                in0=picked[0][:, runs, t0:t1, :],
-                in1=picked[1][:, runs, t0:t1, :],
+                out=z[1][:, t0:t1, c0 - HALF : c1 - HALF].rearrange("p t (b r) -> p b t r", r=RUN),
+                in0=picked[0][:, runs, :, :],
+                in1=picked[1][:, runs, :, :],
                 op=ALU.max,
             )
 
         def interleave(c0, c1):
             nc.scalar.copy(
                 out=z_b[:, c0:c1, :].rearrange("p (c i) t -> p c t i", i=4),
-                in_=z[:, :, c0:c1].rearrange("p t (c i) -> p c t i", i=4),
+                in_=z[c0 // HALF][:, :, c0 % HALF : (c1 - 1) % HALF + 1].rearrange("p t (c i) -> p c t i", i=4),
             )
 
         accs = {}
 
-        def own_pass(c0, c1):
-            accs[c0] = psum.tile([P, HALF], F32, name="out_acc", tag=f"bank{(4 + len(accs)) % 8}")
+        def second_layer(c0, c1, which):
+            first = c0 not in accs
+            if first:
+                accs[c0] = psum.tile([P, HALF], F32, name="out_acc", tag=f"bank{(4 + len(accs)) % 8}")
+            codes_in, scales_in = ((h_q, h_sc), (z_q, z_sc))[which]
             nc.tensor.matmul_mx(
                 out=accs[c0][:, : c1 - c0],
-                lhsT=w23[:, 0:N].bitcast(FP8X4),
-                lhsT_scale=w23_sc[:, 0:N],
-                rhs=h_q[:, c0:c1].bitcast(FP8X4),
-                rhs_scale=h_sc[:, c0:c1],
-                start=True,
-                stop=False,
+                lhsT=w23[:, which * N : (which + 1) * N].bitcast(FP8X4),
+                lhsT_scale=w23_sc[:, which * N : (which + 1) * N],
+                rhs=codes_in[:, c0:c1].bitcast(FP8X4),
+                rhs_scale=scales_in[:, c0:c1],
+                start=first,
+                stop=not first,
             )
 
-        def finish(c0, c1):
-            quantize(z_q, z_sc, z_b, c0, c1)
-            nc.tensor.matmul_mx(
-                out=accs[c0][:, : c1 - c0],
-                lhsT=w23[:, N : 2 * N].bitcast(FP8X4),
-                lhsT_scale=w23_sc[:, N : 2 * N],
-                rhs=z_q[:, c0:c1].bitcast(FP8X4),
-                rhs_scale=z_sc[:, c0:c1],
-                start=False,
-                stop=True,
-            )
+        def own(c0):
+            quantize(h_q, h_sc, h_b[c0 // QUARTER][:], c0, c0 + QUARTER)
+            for s0, s1 in spans:
+                if c0 <= s0 < c0 + QUARTER:
+                    second_layer(s0, s1, 0)
+
+        def neighbours(c0, c1):
+            quantize(z_q, z_sc, z_b[:, c0:c1, :], c0, c1)
+            second_layer(c0, c1, 1)
 
         def store(c0, c1):
             if c1 - c0 > P:
@@ -203,54 +200,56 @@ def tile_picked_wsagecat_maxrelu_l_kernel(
 
         edges = [sum(CHUNKS[:n]) for n in range(len(CHUNKS) + 1)]
         spans = list(zip(edges[:-1], edges[1:]))
-        diff = keep.tile([P, 2, 2, QUARTER], F32, name="diff", align_bytes=64)
-        units = [(0, 0), (0, HALF), (1, HALF), (1, 0)]
+        units = [(0, 0), (1, 0), (2, 0), (3, 0), (0, HALF), (1, HALF)]
         pairs = []
+        excess = []
 
         def add_back(u):
             t, c0 = units[u]
             nc.gpsimd.tensor_tensor(
-                out=z[:, t, c0 : c0 + HALF].rearrange("p (b r) -> p b r", b=2),
-                in0=diff[:, u % 2, :, :],
+                out=z[c0 // HALF][:, t, :].rearrange("p (b r) -> p b r", b=2),
+                in0=excess[u][:],
                 in1=pairs[u][:, :, 1, :],
                 op=ALU.add,
             )
 
         for u, (t, c0) in enumerate(units):
-            pair = h_flat[:, u * T : (u + 1) * T].rearrange("p (b d r) -> p b d r", b=2, d=2)
+            pair = keep.tile([P, 2, 2, QUARTER], BF16, name=f"pair{u}", tag=f"pair{u % 4}", align_bytes=64)
             pairs.append(pair)
             for d in range(2):
                 nc.vector.tensor_copy(
                     out=pair[:, :, d, :],
                     in_=h[:, t * T : (t + 1) * T].indirect(lists[d][:, c0 // 16 : (c0 + HALF) // 16]),
                 )
-            nc.gpsimd.tensor_tensor(
-                out=diff[:, u % 2, :, :], in0=pair[:, :, 0, :], in1=pair[:, :, 1, :], op=ALU.subtract
-            )
-            nc.scalar.activation(out=diff[:, u % 2, :, :], in_=diff[:, u % 2, :, :], func=ACT.Relu)
+            diff = keep.tile([P, 2, QUARTER], F32, name=f"diff{u}", tag=f"work{u}", align_bytes=64)
+            nc.gpsimd.tensor_tensor(out=diff[:], in0=pair[:, :, 0, :], in1=pair[:, :, 1, :], op=ALU.subtract)
+            excess.append(keep.tile([P, 2, QUARTER], F32, name=f"excess{u}", tag=f"work{u + 2}", align_bytes=64))
+            nc.scalar.activation(out=excess[u][:], in_=diff[:], func=ACT.Relu)
+            if u < 4:
+                interleave_h(u, f"work{u}")
             if u > 0:
                 add_back(u - 1)
         add_back(len(units) - 1)
-        for a in range(4):
-            interleave_h(a)
-        gather(0, 2, 0, T)
-        gather(1, 2, 0, HALF)
-        gather(0, 3, 0, HALF)
-        gather(1, 3, 0, HALF)
-        gather(1, 2, HALF, T)
-        largest(2, 4, 0, HALF)
+        for d in range(2):
+            picked.append(keep.tile([P, HALF // RUN, 2, RUN], BF16, name=f"picked{d}", tag=f"pair{2 + d}", align_bytes=64))
+        gather(0, 2, HALF, T)
         gather(0, 3, HALF, T)
+        gather(1, 2, HALF, T)
         gather(1, 3, HALF, HALF + QUARTER)
         gather(1, 3, HALF + QUARTER, T)
         largest(2, 4, HALF, HALF + QUARTER)
         largest(2, 4, HALF + QUARTER, T)
         for span in spans:
             interleave(*span)
-        for c0 in range(0, T, QUARTER):
-            quantize(h_q, h_sc, h_b, c0, c0 + QUARTER)
-        for span in spans:
-            own_pass(*span)
-        for span in spans:
-            finish(*span)
+        h_q = keep.tile([P, T], U32, name="h_q", tag="work7", align_bytes=64)
+        z_q = keep.tile([P, T], U32, name="z_q", tag="pair1", align_bytes=64)
+        for c0, c1 in spans[:2]:
+            neighbours(c0, c1)
+            own(c0)
+        own(spans[2][0])
+        own(spans[3][0])
+        for span in spans[2:]:
+            neighbours(*span)
+        res = keep.tile([P, T], F32, name="res", tag="z1", align_bytes=64)
         for span in spans:
             store(*span)

@@ -19,7 +19,6 @@ P = 128
 PACK = 4
 HALF = 512
 QUARTER = 256
-RUN = 64
 CHUNKS = (256, 256, 256, 128, 128)
 
 
@@ -138,24 +137,13 @@ def tile_picked_wsagecat_maxrelu_l_kernel(
                 in_=values.rearrange("p c t -> p (c t)"),
             )
 
-        picked = []
         z = [keep.tile([P, PACK, HALF], BF16, name=f"z{n}", tag=f"z{n}", align_bytes=64) for n in range(2)]
         z_b = keep.tile([P, T, PACK], BF16, name="z_b", align_bytes=64)
         z_sc = keep.tile([P, T], U8, name="z_sc", align_bytes=64)
 
-        def gather(d, t, c0, c1):
+        def gather(d, t, c0, c1, dst):
             nc.vector.tensor_copy(
-                out=picked[d][:, (c0 - HALF) // RUN : (c1 - HALF) // RUN, t - 2, :],
-                in_=h[:, t * T : (t + 1) * T].indirect(lists[d][:, c0 // 16 : c1 // 16]),
-            )
-
-        def largest(t0, t1, c0, c1):
-            runs = slice((c0 - HALF) // RUN, (c1 - HALF) // RUN)
-            nc.vector.tensor_tensor(
-                out=z[1][:, t0:t1, c0 - HALF : c1 - HALF].rearrange("p t (b r) -> p b t r", r=RUN),
-                in0=picked[0][:, runs, :, :],
-                in1=picked[1][:, runs, :, :],
-                op=ALU.max,
+                out=dst, in_=h[:, t * T : (t + 1) * T].indirect(lists[d][:, c0 // 16 : c1 // 16])
             )
 
         def interleave(c0, c1):
@@ -200,56 +188,57 @@ def tile_picked_wsagecat_maxrelu_l_kernel(
 
         edges = [sum(CHUNKS[:n]) for n in range(len(CHUNKS) + 1)]
         spans = list(zip(edges[:-1], edges[1:]))
-        units = [(0, 0), (1, 0), (2, 0), (3, 0), (0, HALF), (1, HALF)]
-        pairs = []
         excess = []
+        kept = []
+        targets = []
 
         def add_back(u):
-            t, c0 = units[u]
-            nc.gpsimd.tensor_tensor(
-                out=z[c0 // HALF][:, t, :].rearrange("p (b r) -> p b r", b=2),
-                in0=excess[u][:],
-                in1=pairs[u][:, :, 1, :],
-                op=ALU.add,
-            )
+            nc.gpsimd.tensor_tensor(out=targets[u], in0=excess[u][:], in1=kept[u], op=ALU.add)
 
-        for u, (t, c0) in enumerate(units):
-            pair = keep.tile([P, 2, 2, QUARTER], BF16, name=f"pair{u}", tag=f"pair{u % 4}", align_bytes=64)
-            pairs.append(pair)
-            for d in range(2):
-                nc.vector.tensor_copy(
-                    out=pair[:, :, d, :],
-                    in_=h[:, t * T : (t + 1) * T].indirect(lists[d][:, c0 // 16 : (c0 + HALF) // 16]),
-                )
-            diff = keep.tile([P, 2, QUARTER], F32, name=f"diff{u}", tag=f"work{u}", align_bytes=64)
-            nc.gpsimd.tensor_tensor(out=diff[:], in0=pair[:, :, 0, :], in1=pair[:, :, 1, :], op=ALU.subtract)
-            excess.append(keep.tile([P, 2, QUARTER], F32, name=f"excess{u}", tag=f"work{u + 2}", align_bytes=64))
+        def difference(u, first, second, target):
+            shape = [P, 2, first.shape[2]]
+            diff = keep.tile(shape, F32, name=f"diff{u}", tag=f"work{u}", align_bytes=64)
+            nc.gpsimd.tensor_tensor(out=diff[:], in0=first, in1=second, op=ALU.subtract)
+            excess.append(keep.tile(shape, F32, name=f"excess{u}", tag=f"work{u + 2}", align_bytes=64))
             nc.scalar.activation(out=excess[u][:], in_=diff[:], func=ACT.Relu)
+            kept.append(second)
+            targets.append(target.rearrange("p (b r) -> p b r", b=2))
             if u < 4:
                 interleave_h(u, f"work{u}")
             if u > 0:
                 add_back(u - 1)
-        add_back(len(units) - 1)
+
+        for u, (t, c0) in enumerate([(0, 0), (1, 0), (2, 0), (3, 0), (0, HALF)]):
+            pair = keep.tile([P, 2, 2, QUARTER], BF16, name=f"pair{u}", tag=f"pair{u % 4}", align_bytes=64)
+            for d in range(2):
+                gather(d, t, c0, c0 + HALF, pair[:, :, d, :])
+            difference(u, pair[:, :, 0, :], pair[:, :, 1, :], z[c0 // HALF][:, t, :])
+
+        picked = keep.tile([P, 2, 4, 3, P], BF16, name="picked", tag="pair1", align_bytes=64)
         for d in range(2):
-            picked.append(keep.tile([P, HALF // RUN, 2, RUN], BF16, name=f"picked{d}", tag=f"pair{2 + d}", align_bytes=64))
-        gather(0, 2, HALF, T)
-        gather(0, 3, HALF, T)
-        gather(1, 2, HALF, T)
-        gather(1, 3, HALF, HALF + QUARTER)
-        gather(1, 3, HALF + QUARTER, T)
-        largest(2, 4, HALF, HALF + QUARTER)
-        largest(2, 4, HALF + QUARTER, T)
+            gather(d, 1, HALF, T, picked[:, d, :, 0, :])
+        difference(5, picked[:, 0, 0:2, 0, :], picked[:, 1, 0:2, 0, :], z[1][:, 1, 0:QUARTER])
+        add_back(5)
+        gather(0, 2, HALF, T, picked[:, 0, :, 1, :])
+        gather(0, 3, HALF, T, picked[:, 0, :, 2, :])
+        gather(1, 2, HALF, T, picked[:, 1, :, 1, :])
+        gather(1, 3, HALF, HALF + QUARTER, picked[:, 1, 0:2, 2, :])
+        gather(1, 3, HALF + QUARTER, T, picked[:, 1, 2:4, 2, :])
+        for q, t0 in ((0, 2), (1, 1)):
+            nc.vector.tensor_tensor(
+                out=z[1][:, t0:, q * QUARTER : (q + 1) * QUARTER].rearrange("p t (b r) -> p b t r", b=2),
+                in0=picked[:, 0, 2 * q : 2 * q + 2, t0 - 1 :, :],
+                in1=picked[:, 1, 2 * q : 2 * q + 2, t0 - 1 :, :],
+                op=ALU.max,
+            )
         for span in spans:
             interleave(*span)
         h_q = keep.tile([P, T], U32, name="h_q", tag="work7", align_bytes=64)
         z_q = keep.tile([P, T], U32, name="z_q", tag="pair1", align_bytes=64)
-        for c0, c1 in spans[:2]:
-            neighbours(c0, c1)
+        for c0, c1 in spans[:4]:
             own(c0)
-        own(spans[2][0])
-        own(spans[3][0])
-        for span in spans[2:]:
-            neighbours(*span)
+            neighbours(c0, c1)
+        neighbours(*spans[4])
         res = keep.tile([P, T], F32, name="res", tag="z1", align_bytes=64)
         for span in spans:
             store(*span)

@@ -28,6 +28,7 @@ def tile_picked_wsagecat_maxrelu_l_kernel(
     nc = tc.nc
     with ExitStack() as ctx:
         keep = ctx.enter_context(tc.tile_pool(name="keep", bufs=1))
+        shared = ctx.enter_context(tc.tile_pool(name="shared", bufs=1))
         psum = ctx.enter_context(tc.psum_pool(name="psum", bufs=1))
 
         def load_scales(tile, cols, src):
@@ -77,40 +78,45 @@ def tile_picked_wsagecat_maxrelu_l_kernel(
             )
 
         nc.vector.tensor_copy(out=w1_dst[:, : P // 2, :, :], in_=lo_src)
-        nc.vector.tensor_copy(out=w1_dst[:, P // 2 :, 0, :], in_=hi_src[:, :, 0, :])
-        nc.scalar.activation(out=w1_dst[:, P // 2 :, 1:4, :], in_=hi_src[:, :, 1:4, :], func=ACT.Copy)
-        quant_w1(0, 1)
+        nc.vector.tensor_copy(out=w1_dst[:, P // 2 :, 1, :], in_=hi_src[:, :, 1, :])
+        nc.scalar.activation(out=w1_dst[:, P // 2 :, 0, :], in_=hi_src[:, :, 0, :], func=ACT.Copy)
+        nc.scalar.activation(out=w1_dst[:, P // 2 :, 2:4, :], in_=hi_src[:, :, 2:4, :], func=ACT.Copy)
         quant_w1(1, 2)
+        quant_w1(0, 1)
         quant_w1(2, 4)
 
-        h = keep.tile([P, PACK * T], F32, name="h", align_bytes=64)
+        pairs = [keep.tile([P, 2 * T], F32, name=f"h_pair{u}", align_bytes=64) for u in range(2)]
+
+        def plane(t):
+            return pairs[t // 2][:, (t % 2) * T : (t % 2 + 1) * T]
 
         filled = []
 
-        def first_layer(t):
-            width = QUARTER if t == 0 else HALF
-            for c0 in range(0, T, width):
-                acc = psum.tile([P, HALF], F32, name="h_acc", tag=f"bank{len(filled) % 4}")
-                filled.append(acc)
-                for a in range(c0 // QUARTER, (c0 + width) // QUARTER):
-                    cols = slice(a * QUARTER, (a + 1) * QUARTER)
-                    nc.tensor.matmul_mx(
-                        out=acc[:, a * QUARTER - c0 : (a + 1) * QUARTER - c0],
-                        lhsT=w1_q[:, t * P : (t + 1) * P].bitcast(FP8X4),
-                        lhsT_scale=w1_sc[:, t * P : (t + 1) * P],
-                        rhs=x_w[:, cols].bitcast(FP8X4),
-                        rhs_scale=x_sc[4 * a :, :],
-                        start=True,
-                        stop=True,
-                    )
-                dst = h[:, t * T + c0 : t * T + c0 + width]
-                if t == 0 and c0 % HALF == 0:
-                    nc.vector.tensor_scalar_max(out=dst, in0=acc[:, :width], scalar1=0.0)
-                else:
-                    nc.scalar.activation(out=dst, in_=acc[:, :width], func=ACT.Relu)
+        def first_layer(t, c0, width, on_vector):
+            acc = psum.tile([P, HALF], F32, name="h_acc", tag=f"bank{len(filled) % 4}")
+            filled.append(acc)
+            for a in range(c0 // QUARTER, (c0 + width) // QUARTER):
+                cols = slice(a * QUARTER, (a + 1) * QUARTER)
+                nc.tensor.matmul_mx(
+                    out=acc[:, a * QUARTER - c0 : (a + 1) * QUARTER - c0],
+                    lhsT=w1_q[:, t * P : (t + 1) * P].bitcast(FP8X4),
+                    lhsT_scale=w1_sc[:, t * P : (t + 1) * P],
+                    rhs=x_w[:, cols].bitcast(FP8X4),
+                    rhs_scale=x_sc[4 * a :, :],
+                    start=True,
+                    stop=True,
+                )
+            dst = plane(t)[:, c0 : c0 + width]
+            if on_vector:
+                nc.vector.tensor_scalar_max(out=dst, in0=acc[:, :width], scalar1=0.0)
+            else:
+                nc.scalar.activation(out=dst, in_=acc[:, :width], func=ACT.Relu)
 
-        for t in range(PACK):
-            first_layer(t)
+        for c0 in range(0, T, QUARTER):
+            first_layer(1, c0, QUARTER, c0 % HALF == 0)
+        for t in (0, 3, 2):
+            for c0 in (0, HALF):
+                first_layer(t, c0, HALF, False)
 
         w23 = keep.tile([P, 2 * N], U32, name="w23", tag="w1_raw", align_bytes=64)
         w23_sc = keep.tile([P, 2 * N], U8, name="w23_sc", tag="w1_b", align_bytes=64)
@@ -120,36 +126,61 @@ def tile_picked_wsagecat_maxrelu_l_kernel(
         load_scales(w23_sc, slice(0, N), w2_scales)
         load_scales(w23_sc, slice(N, 2 * N), w3_scales)
 
-        h_b = []
-        h_sc = keep.tile([P, T], U8, name="h_sc", align_bytes=64)
-        h_src = h[:].rearrange("p (t c i) -> p c t i", t=PACK, i=4)
+        column = PACK * 2
+        h_b = [
+            shared.tile([P, HALF, PACK], BF16, name=f"h_b{n}", offset=n * HALF * column, align_bytes=64)
+            for n in range(2)
+        ]
 
-        def interleave_h(a, room):
-            groups = slice(a * QUARTER // 4, (a + 1) * QUARTER // 4)
-            tile = keep.tile([P, QUARTER, PACK], BF16, name=f"h_b{a}", tag=room, align_bytes=64)
-            h_b.append(tile)
-            nc.scalar.copy(out=tile[:].rearrange("p (c i) t -> p c t i", i=4), in_=h_src[:, groups, :, :])
+        def interleave_h(u, n):
+            nc.gpsimd.tensor_scalar(
+                out=h_b[n][:, :, 2 * u : 2 * u + 2],
+                in0=pairs[u][:].rearrange("p (l c) -> p c l", l=2)[:, n * HALF : (n + 1) * HALF, :],
+                scalar1=1.0,
+                scalar2=0.0,
+                op0=ALU.mult,
+                op1=ALU.add,
+            )
+
+        for u in range(2):
+            for n in range(2):
+                interleave_h(u, n)
+
+        def gather_vector(d, t, n, dst):
+            nc.vector.tensor_copy(out=dst, in_=plane(t).indirect(lists[d][:, n * HALF // 16 : (n + 1) * HALF // 16]))
+
+        def gather_scalar(d, u, q, dst):
+            nc.scalar.activation(
+                out=dst,
+                in_=pairs[u][:].indirect(lists[d][:, q * QUARTER // 16 : (q + 1) * QUARTER // 16]),
+                func=ACT.Copy,
+            )
+
+        low = [keep.tile([P, 2, PACK, QUARTER], BF16, name=f"low{d}", align_bytes=64) for d in range(2)]
+        high1 = keep.tile([P, 2, 2, QUARTER], BF16, name="high1", align_bytes=64)
+        high_even = keep.tile([P, 2, 2, 2, QUARTER], BF16, name="high_even", align_bytes=64)
+        for d in range(2):
+            gather_vector(d, 1, 0, low[d][:, :, 1, :])
+        for d in range(2):
+            gather_vector(d, 1, 1, high1[:, :, d, :])
+        for d in range(2):
+            gather_vector(d, 3, 0, low[d][:, :, 3, :])
+        for q in range(4):
+            for u in range(2):
+                for d in range(2):
+                    gather_scalar(d, u, q, low[d][:, q, 2 * u, :] if q < 2 else high_even[:, q - 2, d, u, :])
+
+        h_q = keep.tile([P, T], U32, name="h_q", align_bytes=64)
+        h_sc = keep.tile([P, T], U8, name="h_sc", align_bytes=64)
+        z_q = keep.tile([P, T], U32, name="z_q", align_bytes=64)
+        z_sc = keep.tile([P, T], U8, name="z_sc", align_bytes=64)
+        res = keep.tile([P, T], F32, name="res", align_bytes=64)
 
         def quantize(codes, scales, values, c0, c1):
             nc.vector.quantize_mx(
                 out=codes[:, c0:c1].bitcast(FP8X4),
                 scales=scales[:, c0:c1],
                 in_=values.rearrange("p c t -> p (c t)"),
-            )
-
-        z = [keep.tile([P, PACK, HALF], BF16, name=f"z{n}", tag=f"z{n}", align_bytes=64) for n in range(2)]
-        z_b = keep.tile([P, T, PACK], BF16, name="z_b", align_bytes=64)
-        z_sc = keep.tile([P, T], U8, name="z_sc", align_bytes=64)
-
-        def gather(d, t, c0, c1, dst):
-            nc.vector.tensor_copy(
-                out=dst, in_=h[:, t * T : (t + 1) * T].indirect(lists[d][:, c0 // 16 : c1 // 16])
-            )
-
-        def interleave(c0, c1):
-            nc.scalar.copy(
-                out=z_b[:, c0:c1, :].rearrange("p (c i) t -> p c t i", i=4),
-                in_=z[c0 // HALF][:, :, c0 % HALF : (c1 - 1) % HALF + 1].rearrange("p t (c i) -> p c t i", i=4),
             )
 
         accs = {}
@@ -169,76 +200,84 @@ def tile_picked_wsagecat_maxrelu_l_kernel(
                 stop=not first,
             )
 
+        edges = [sum(CHUNKS[:n]) for n in range(len(CHUNKS) + 1)]
+        spans = list(zip(edges[:-1], edges[1:]))
+        z_b = {}
+
         def own(c0):
-            quantize(h_q, h_sc, h_b[c0 // QUARTER][:], c0, c0 + QUARTER)
+            quantize(h_q, h_sc, h_b[c0 // HALF][:], c0, c0 + HALF)
             for s0, s1 in spans:
-                if c0 <= s0 < c0 + QUARTER:
+                if c0 <= s0 < c0 + HALF:
                     second_layer(s0, s1, 0)
 
+        def largest(dst, first, second):
+            nc.vector.tensor_tensor(out=dst, in0=first, in1=second, op=ALU.max)
+
+        def interleave(copy, planes, c0, c1):
+            z_b[c0] = keep.tile([P, c1 - c0, PACK], BF16, name=f"z_b{c0}", align_bytes=64)
+            copy(
+                out=z_b[c0][:].rearrange("p (c i) t -> p c t i", i=4),
+                in_=planes.rearrange("p t (c i) -> p c t i", i=4),
+            )
+
         def neighbours(c0, c1):
-            quantize(z_q, z_sc, z_b[:, c0:c1, :], c0, c1)
+            quantize(z_q, z_sc, z_b[c0][:], c0, c1)
             second_layer(c0, c1, 1)
 
         def store(c0, c1):
-            if c1 - c0 > P:
+            if c1 < T:
                 nc.scalar.activation(out=res[:, c0:c1], in_=accs[c0][:, : c1 - c0], func=ACT.Relu)
             else:
                 nc.vector.tensor_scalar_max(out=res[:, c0:c1], in0=accs[c0][:, : c1 - c0], scalar1=0.0)
             nc.sync.dma_start(out=out[:, c0:c1], in_=res[:, c0:c1])
 
-        edges = [sum(CHUNKS[:n]) for n in range(len(CHUNKS) + 1)]
-        spans = list(zip(edges[:-1], edges[1:]))
-        excess = []
-        kept = []
-        targets = []
-
-        def add_back(u):
-            nc.gpsimd.tensor_tensor(out=targets[u], in0=excess[u][:], in1=kept[u], op=ALU.add)
-
-        def difference(u, first, second, target):
-            shape = [P, 2, first.shape[2]]
-            diff = keep.tile(shape, F32, name=f"diff{u}", tag=f"work{u}", align_bytes=64)
-            nc.gpsimd.tensor_tensor(out=diff[:], in0=first, in1=second, op=ALU.subtract)
-            excess.append(keep.tile(shape, F32, name=f"excess{u}", tag=f"work{u + 2}", align_bytes=64))
-            nc.scalar.activation(out=excess[u][:], in_=diff[:], func=ACT.Relu)
-            kept.append(second)
-            targets.append(target.rearrange("p (b r) -> p b r", b=2))
-            if u < 4:
-                interleave_h(u, f"work{u}")
-            if u > 0:
-                add_back(u - 1)
-
-        for u, (t, c0) in enumerate([(0, 0), (1, 0), (2, 0), (3, 0), (0, HALF)]):
-            pair = keep.tile([P, 2, 2, QUARTER], BF16, name=f"pair{u}", tag=f"pair{u % 4}", align_bytes=64)
-            for d in range(2):
-                gather(d, t, c0, c0 + HALF, pair[:, :, d, :])
-            difference(u, pair[:, :, 0, :], pair[:, :, 1, :], z[c0 // HALF][:, t, :])
-
-        picked = keep.tile([P, 2, 4, 3, P], BF16, name="picked", tag="pair1", align_bytes=64)
+        own(0)
+        own(HALF)
+        z_low = []
+        for q in range(2):
+            tile = shared.tile([P, PACK, QUARTER], BF16, name=f"z{q}", offset=q * QUARTER * column, align_bytes=64)
+            z_low.append(tile)
+            largest(tile[:], low[0][:, q, :, :], low[1][:, q, :, :])
+        high3 = shared.tile([P, 2, 2, QUARTER], BF16, name="high3", offset=HALF * column, align_bytes=64)
         for d in range(2):
-            gather(d, 1, HALF, T, picked[:, d, :, 0, :])
-        difference(5, picked[:, 0, 0:2, 0, :], picked[:, 1, 0:2, 0, :], z[1][:, 1, 0:QUARTER])
-        add_back(5)
-        gather(0, 2, HALF, T, picked[:, 0, :, 1, :])
-        gather(0, 3, HALF, T, picked[:, 0, :, 2, :])
-        gather(1, 2, HALF, T, picked[:, 1, :, 1, :])
-        gather(1, 3, HALF, HALF + QUARTER, picked[:, 1, 0:2, 2, :])
-        gather(1, 3, HALF + QUARTER, T, picked[:, 1, 2:4, 2, :])
-        for q, t0 in ((0, 2), (1, 1)):
-            nc.vector.tensor_tensor(
-                out=z[1][:, t0:, q * QUARTER : (q + 1) * QUARTER].rearrange("p t (b r) -> p b t r", b=2),
-                in0=picked[:, 0, 2 * q : 2 * q + 2, t0 - 1 :, :],
-                in1=picked[:, 1, 2 * q : 2 * q + 2, t0 - 1 :, :],
-                op=ALU.max,
+            gather_vector(d, 3, 1, high3[:, :, d, :])
+        for q in range(2):
+            c0 = q * QUARTER
+            z_b[c0] = shared.tile([P, QUARTER, PACK], BF16, name=f"z_b{c0}", offset=(T + c0) * column, align_bytes=64)
+            nc.gpsimd.tensor_scalar(
+                out=z_b[c0][:],
+                in0=z_low[q][:].rearrange("p t c -> p c t"),
+                scalar1=1.0,
+                scalar2=0.0,
+                op0=ALU.mult,
+                op1=ALU.add,
             )
-        for span in spans:
-            interleave(*span)
-        h_q = keep.tile([P, T], U32, name="h_q", tag="work7", align_bytes=64)
-        z_q = keep.tile([P, T], U32, name="z_q", tag="pair1", align_bytes=64)
-        for c0, c1 in spans[:4]:
-            own(c0)
-            neighbours(c0, c1)
+        neighbours(*spans[0])
+        neighbours(*spans[1])
+
+        z_high = shared.tile([P, 2, PACK, QUARTER], BF16, name="z_high", offset=T * column, align_bytes=64)
+        largest(z_high[:, :, 1, :], high1[:, :, 0, :], high1[:, :, 1, :])
+        largest(z_high[:, :, 3, :], high3[:, :, 0, :], high3[:, :, 1, :])
+
+        def piece(c0, c1):
+            return c0 // QUARTER - 2, slice(c0 % QUARTER, (c1 - 1) % QUARTER + 1)
+
+        def largest_even(c0, c1):
+            q, cols = piece(c0, c1)
+            largest(z_high[:, q, 0:PACK:2, cols], high_even[:, q, 0, :, cols], high_even[:, q, 1, :, cols])
+
+        def interleave_high(copy, c0, c1):
+            q, cols = piece(c0, c1)
+            interleave(copy, z_high[:, q, :, cols], c0, c1)
+
+        largest_even(*spans[2])
+        largest_even(*spans[3])
+        interleave_high(nc.vector.tensor_copy, *spans[2])
+        interleave_high(nc.scalar.copy, *spans[3])
+        largest_even(*spans[4])
+        neighbours(*spans[2])
+        interleave_high(nc.vector.tensor_copy, *spans[4])
+        neighbours(*spans[3])
         neighbours(*spans[4])
-        res = keep.tile([P, T], F32, name="res", tag="z1", align_bytes=64)
         for span in spans:
             store(*span)

@@ -19,7 +19,8 @@ P = 128
 PACK = 4
 HALF = 512
 QUARTER = 256
-CHUNKS = (256, 256, 256, 128, 128)
+CHUNKS = (512, 256, 128, 128)
+ON_GPSIMD = 384
 
 
 def tile_picked_wsagecat_maxrelu_l_kernel(
@@ -43,11 +44,11 @@ def tile_picked_wsagecat_maxrelu_l_kernel(
 
         x_sc = keep.tile([P, QUARTER], U8, name="x_sc", align_bytes=64)
         nc.vector.memset(x_sc[:].bitcast(U32), 0)
-        w1_raw = keep.tile([P, PACK, H // 2], F32, name="w1_raw", tag="w1_raw", align_bytes=64)
-        w1_hi = keep.tile([P, PACK, H // 2], F32, name="w1_hi", align_bytes=64)
+        w1_raw = keep.tile([P, 2, H], F32, name="w1_raw", tag="w1_raw", align_bytes=64)
+        w1_hi = keep.tile([P, 2, H], F32, name="w1_hi", align_bytes=64)
         w1_rows = w1.rearrange("(p j) c -> p j c", j=PACK)
-        nc.sync.dma_start(out=w1_raw[:], in_=w1_rows[:, :, : H // 2])
-        nc.sync.dma_start(out=w1_hi[:], in_=w1_rows[:, :, H // 2 :])
+        nc.sync.dma_start(out=w1_raw[:], in_=w1_rows[:, :2, :])
+        nc.sync.dma_start(out=w1_hi[:], in_=w1_rows[:, 2:, :])
         for q in range(4):
             nc.sync.dma_start(
                 out=x_sc[32 * q : 32 * q + 16, :].bitcast(I32),
@@ -77,10 +78,10 @@ def tile_picked_wsagecat_maxrelu_l_kernel(
                 in_=w1_b[:, t0:t1, :, :].rearrange("p t m j -> p (t m j)"),
             )
 
-        nc.vector.tensor_copy(out=w1_dst[:, : P // 2, :, :], in_=lo_src)
-        nc.vector.tensor_copy(out=w1_dst[:, P // 2 :, 1, :], in_=hi_src[:, :, 1, :])
-        nc.scalar.activation(out=w1_dst[:, P // 2 :, 0, :], in_=hi_src[:, :, 0, :], func=ACT.Copy)
-        nc.scalar.activation(out=w1_dst[:, P // 2 :, 2:4, :], in_=hi_src[:, :, 2:4, :], func=ACT.Copy)
+        nc.vector.tensor_copy(out=w1_dst[:, :, :, :2], in_=lo_src)
+        nc.vector.tensor_copy(out=w1_dst[:, :, 1, 2:], in_=hi_src[:, :, 1, :])
+        nc.vector.tensor_copy(out=w1_dst[:, :, 0, 2:], in_=hi_src[:, :, 0, :])
+        nc.scalar.activation(out=w1_dst[:, :, 2:4, 2:], in_=hi_src[:, :, 2:4, :], func=ACT.Copy)
         quant_w1(1, 2)
         quant_w1(0, 1)
         quant_w1(2, 4)
@@ -233,27 +234,26 @@ def tile_picked_wsagecat_maxrelu_l_kernel(
 
         own(0)
         own(HALF)
-        z_low = []
+        z_low = shared.tile([P, PACK, HALF], BF16, name="z_low", offset=0, align_bytes=64)
         for q in range(2):
-            tile = shared.tile([P, PACK, QUARTER], BF16, name=f"z{q}", offset=q * QUARTER * column, align_bytes=64)
-            z_low.append(tile)
-            largest(tile[:], low[0][:, q, :, :], low[1][:, q, :, :])
+            largest(z_low[:, :, q * QUARTER : (q + 1) * QUARTER], low[0][:, q, :, :], low[1][:, q, :, :])
         high3 = shared.tile([P, 2, 2, QUARTER], BF16, name="high3", offset=HALF * column, align_bytes=64)
         for d in range(2):
             gather_vector(d, 3, 1, high3[:, :, d, :])
-        for q in range(2):
-            c0 = q * QUARTER
-            z_b[c0] = shared.tile([P, QUARTER, PACK], BF16, name=f"z_b{c0}", offset=(T + c0) * column, align_bytes=64)
-            nc.gpsimd.tensor_scalar(
-                out=z_b[c0][:],
-                in0=z_low[q][:].rearrange("p t c -> p c t"),
-                scalar1=1.0,
-                scalar2=0.0,
-                op0=ALU.mult,
-                op1=ALU.add,
-            )
+        z_b[0] = shared.tile([P, HALF, PACK], BF16, name="z_b0", offset=T * column, align_bytes=64)
+        nc.gpsimd.tensor_scalar(
+            out=z_b[0][:, :ON_GPSIMD, :],
+            in0=z_low[:, :, :ON_GPSIMD].rearrange("p t c -> p c t"),
+            scalar1=1.0,
+            scalar2=0.0,
+            op0=ALU.mult,
+            op1=ALU.add,
+        )
+        nc.vector.tensor_copy(
+            out=z_b[0][:, ON_GPSIMD:, :].rearrange("p (c i) t -> p c t i", i=4),
+            in_=z_low[:, :, ON_GPSIMD:].rearrange("p t (c i) -> p c t i", i=4),
+        )
         neighbours(*spans[0])
-        neighbours(*spans[1])
 
         z_high = shared.tile([P, 2, PACK, QUARTER], BF16, name="z_high", offset=T * column, align_bytes=64)
         largest(z_high[:, :, 1, :], high1[:, :, 0, :], high1[:, :, 1, :])
@@ -270,14 +270,14 @@ def tile_picked_wsagecat_maxrelu_l_kernel(
             q, cols = piece(c0, c1)
             interleave(copy, z_high[:, q, :, cols], c0, c1)
 
+        largest_even(*spans[1])
         largest_even(*spans[2])
+        interleave_high(nc.vector.tensor_copy, *spans[1])
+        interleave_high(nc.scalar.copy, *spans[2])
         largest_even(*spans[3])
-        interleave_high(nc.vector.tensor_copy, *spans[2])
-        interleave_high(nc.scalar.copy, *spans[3])
-        largest_even(*spans[4])
+        neighbours(*spans[1])
+        interleave_high(nc.vector.tensor_copy, *spans[3])
         neighbours(*spans[2])
-        interleave_high(nc.vector.tensor_copy, *spans[4])
         neighbours(*spans[3])
-        neighbours(*spans[4])
         for span in spans:
             store(*span)

@@ -20,7 +20,7 @@ PACK = 4
 HALF = 512
 QUARTER = 256
 CHUNKS = (512, 256, 128, 128)
-ON_GPSIMD = 384
+ON_VECTOR = 96
 
 
 def tile_picked_wsagecat_maxrelu_l_kernel(
@@ -44,11 +44,11 @@ def tile_picked_wsagecat_maxrelu_l_kernel(
 
         x_sc = keep.tile([P, QUARTER], U8, name="x_sc", align_bytes=64)
         nc.vector.memset(x_sc[:].bitcast(U32), 0)
-        w1_raw = keep.tile([P, 2, H], F32, name="w1_raw", tag="w1_raw", align_bytes=64)
-        w1_hi = keep.tile([P, 2, H], F32, name="w1_hi", align_bytes=64)
+        w1_raw = keep.tile([P, PACK, H // 2], F32, name="w1_raw", tag="w1_raw", align_bytes=64)
+        w1_hi = keep.tile([P, PACK, H // 2], F32, name="w1_hi", align_bytes=64)
         w1_rows = w1.rearrange("(p j) c -> p j c", j=PACK)
-        nc.sync.dma_start(out=w1_raw[:], in_=w1_rows[:, :2, :])
-        nc.sync.dma_start(out=w1_hi[:], in_=w1_rows[:, 2:, :])
+        nc.sync.dma_start(out=w1_raw[:], in_=w1_rows[:, :, : H // 2])
+        nc.sync.dma_start(out=w1_hi[:], in_=w1_rows[:, :, H // 2 :])
         for q in range(4):
             nc.sync.dma_start(
                 out=x_sc[32 * q : 32 * q + 16, :].bitcast(I32),
@@ -78,18 +78,19 @@ def tile_picked_wsagecat_maxrelu_l_kernel(
                 in_=w1_b[:, t0:t1, :, :].rearrange("p t m j -> p (t m j)"),
             )
 
-        nc.vector.tensor_copy(out=w1_dst[:, :, :, :2], in_=lo_src)
-        nc.vector.tensor_copy(out=w1_dst[:, :, 1, 2:], in_=hi_src[:, :, 1, :])
-        nc.vector.tensor_copy(out=w1_dst[:, :, 0, 2:], in_=hi_src[:, :, 0, :])
-        nc.scalar.activation(out=w1_dst[:, :, 2:4, 2:], in_=hi_src[:, :, 2:4, :], func=ACT.Copy)
+        nc.vector.tensor_copy(out=w1_dst[:, : P // 2, :, :], in_=lo_src)
+        nc.vector.tensor_copy(out=w1_dst[:, P // 2 :, 1, :], in_=hi_src[:, :, 1, :])
+        nc.vector.tensor_copy(out=w1_dst[:, P // 2 :, 0, :], in_=hi_src[:, :, 0, :])
+        nc.scalar.activation(out=w1_dst[:, P // 2 :, 2:4, :], in_=hi_src[:, :, 2:4, :], func=ACT.Copy)
         quant_w1(1, 2)
-        quant_w1(0, 1)
         quant_w1(2, 4)
+        quant_w1(0, 1)
 
-        pairs = [keep.tile([P, 2 * T], F32, name=f"h_pair{u}", align_bytes=64) for u in range(2)]
+        h = keep.tile([P, PACK * T], F32, name="h", align_bytes=64)
+        copies = {t: keep.tile([P, T], F32, name=f"plane{t}", align_bytes=64) for t in (1, 2)}
 
         def plane(t):
-            return pairs[t // 2][:, (t % 2) * T : (t % 2 + 1) * T]
+            return h[:, t * T : (t + 1) * T]
 
         filled = []
 
@@ -115,9 +116,11 @@ def tile_picked_wsagecat_maxrelu_l_kernel(
 
         for c0 in range(0, T, QUARTER):
             first_layer(1, c0, QUARTER, c0 % HALF == 0)
-        for t in (0, 3, 2):
-            for c0 in (0, HALF):
+        nc.sync.dma_start(out=copies[1][:], in_=plane(1))
+        for c0 in (0, HALF):
+            for t in (2, 3, 0):
                 first_layer(t, c0, HALF, False)
+        nc.sync.dma_start(out=copies[2][:], in_=plane(2))
 
         w23 = keep.tile([P, 2 * N], U32, name="w23", tag="w1_raw", align_bytes=64)
         w23_sc = keep.tile([P, 2 * N], U8, name="w23_sc", tag="w1_b", align_bytes=64)
@@ -128,58 +131,53 @@ def tile_picked_wsagecat_maxrelu_l_kernel(
         load_scales(w23_sc, slice(N, 2 * N), w3_scales)
 
         column = PACK * 2
+        room = HALF * column
         h_b = [
-            shared.tile([P, HALF, PACK], BF16, name=f"h_b{n}", offset=n * HALF * column, align_bytes=64)
+            shared.tile([P, HALF, PACK], BF16, name=f"h_b{n}", offset=n * room, align_bytes=64)
             for n in range(2)
         ]
-
-        def interleave_h(u, n):
+        for n in range(2):
             nc.gpsimd.tensor_scalar(
-                out=h_b[n][:, :, 2 * u : 2 * u + 2],
-                in0=pairs[u][:].rearrange("p (l c) -> p c l", l=2)[:, n * HALF : (n + 1) * HALF, :],
+                out=h_b[n][:],
+                in0=h[:].rearrange("p (t c) -> p c t", t=PACK)[:, n * HALF : (n + 1) * HALF, :],
                 scalar1=1.0,
                 scalar2=0.0,
                 op0=ALU.mult,
                 op1=ALU.add,
             )
 
-        for u in range(2):
-            for n in range(2):
-                interleave_h(u, n)
-
         def gather_vector(d, t, n, dst):
             nc.vector.tensor_copy(out=dst, in_=plane(t).indirect(lists[d][:, n * HALF // 16 : (n + 1) * HALF // 16]))
 
-        def gather_scalar(d, u, q, dst):
+        def gather_scalar(d, t, q, dst):
             nc.scalar.activation(
                 out=dst,
-                in_=pairs[u][:].indirect(lists[d][:, q * QUARTER // 16 : (q + 1) * QUARTER // 16]),
+                in_=copies.get(t, h)[:].indirect(lists[d][:, q * QUARTER // 16 : (q + 1) * QUARTER // 16]),
                 func=ACT.Copy,
             )
 
         low = [keep.tile([P, 2, PACK, QUARTER], BF16, name=f"low{d}", align_bytes=64) for d in range(2)]
-        high1 = keep.tile([P, 2, 2, QUARTER], BF16, name="high1", align_bytes=64)
-        high_even = keep.tile([P, 2, 2, 2, QUARTER], BF16, name="high_even", align_bytes=64)
-        for d in range(2):
-            gather_vector(d, 1, 0, low[d][:, :, 1, :])
-        for d in range(2):
-            gather_vector(d, 1, 1, high1[:, :, d, :])
-        for d in range(2):
-            gather_vector(d, 3, 0, low[d][:, :, 3, :])
-        for q in range(4):
-            for u in range(2):
+        for t in (1, 2, 3):
+            for d in range(2):
+                gather_vector(d, t, 0, low[d][:, :, t, :])
+        for q in range(2):
+            for d in range(2):
+                gather_scalar(d, 0, q, low[d][:, q, 0, :])
+        high = keep.tile([P, 2, 2, 3, QUARTER], BF16, name="high", align_bytes=64)
+        for q in range(2):
+            for t in range(3):
                 for d in range(2):
-                    gather_scalar(d, u, q, low[d][:, q, 2 * u, :] if q < 2 else high_even[:, q - 2, d, u, :])
+                    gather_scalar(d, t, 2 + q, high[:, q, d, t, :])
 
         h_q = keep.tile([P, T], U32, name="h_q", align_bytes=64)
         h_sc = keep.tile([P, T], U8, name="h_sc", align_bytes=64)
-        z_q = keep.tile([P, T], U32, name="z_q", align_bytes=64)
+        z_q = {}
         z_sc = keep.tile([P, T], U8, name="z_sc", align_bytes=64)
         res = keep.tile([P, T], F32, name="res", align_bytes=64)
 
         def quantize(codes, scales, values, c0, c1):
             nc.vector.quantize_mx(
-                out=codes[:, c0:c1].bitcast(FP8X4),
+                out=codes.bitcast(FP8X4),
                 scales=scales[:, c0:c1],
                 in_=values.rearrange("p c t -> p (c t)"),
             )
@@ -190,12 +188,13 @@ def tile_picked_wsagecat_maxrelu_l_kernel(
             first = c0 not in accs
             if first:
                 accs[c0] = psum.tile([P, HALF], F32, name="out_acc", tag=f"bank{(4 + len(accs)) % 8}")
-            codes_in, scales_in = ((h_q, h_sc), (z_q, z_sc))[which]
+            codes_in = z_q[c0][:] if which else h_q[:, c0:c1]
+            scales_in = z_sc if which else h_sc
             nc.tensor.matmul_mx(
                 out=accs[c0][:, : c1 - c0],
                 lhsT=w23[:, which * N : (which + 1) * N].bitcast(FP8X4),
                 lhsT_scale=w23_sc[:, which * N : (which + 1) * N],
-                rhs=codes_in[:, c0:c1].bitcast(FP8X4),
+                rhs=codes_in.bitcast(FP8X4),
                 rhs_scale=scales_in[:, c0:c1],
                 start=first,
                 stop=not first,
@@ -206,7 +205,7 @@ def tile_picked_wsagecat_maxrelu_l_kernel(
         z_b = {}
 
         def own(c0):
-            quantize(h_q, h_sc, h_b[c0 // HALF][:], c0, c0 + HALF)
+            quantize(h_q[:, c0 : c0 + HALF], h_sc, h_b[c0 // HALF][:], c0, c0 + HALF)
             for s0, s1 in spans:
                 if c0 <= s0 < c0 + HALF:
                     second_layer(s0, s1, 0)
@@ -214,15 +213,16 @@ def tile_picked_wsagecat_maxrelu_l_kernel(
         def largest(dst, first, second):
             nc.vector.tensor_tensor(out=dst, in0=first, in1=second, op=ALU.max)
 
-        def interleave(copy, planes, c0, c1):
-            z_b[c0] = keep.tile([P, c1 - c0, PACK], BF16, name=f"z_b{c0}", align_bytes=64)
+        def interleave(copy, planes, c0, c1, tag):
+            z_b[c0] = keep.tile([P, c1 - c0, PACK], BF16, name=f"z_b{c0}", tag=tag, align_bytes=64)
             copy(
                 out=z_b[c0][:].rearrange("p (c i) t -> p c t i", i=4),
                 in_=planes.rearrange("p t (c i) -> p c t i", i=4),
             )
 
         def neighbours(c0, c1):
-            quantize(z_q, z_sc, z_b[c0][:], c0, c1)
+            z_q[c0] = keep.tile([P, c1 - c0], U32, name=f"z_q{c0}", tag=f"z_q{c0}", align_bytes=64)
+            quantize(z_q[c0][:], z_sc, z_b[c0][:], c0, c1)
             second_layer(c0, c1, 1)
 
         def store(c0, c1):
@@ -237,47 +237,47 @@ def tile_picked_wsagecat_maxrelu_l_kernel(
         z_low = shared.tile([P, PACK, HALF], BF16, name="z_low", offset=0, align_bytes=64)
         for q in range(2):
             largest(z_low[:, :, q * QUARTER : (q + 1) * QUARTER], low[0][:, q, :, :], low[1][:, q, :, :])
-        high3 = shared.tile([P, 2, 2, QUARTER], BF16, name="high3", offset=HALF * column, align_bytes=64)
+        z_b[0] = shared.tile([P, HALF, PACK], BF16, name="z_b0", offset=2 * room, align_bytes=64)
+        nc.vector.tensor_copy(
+            out=z_b[0][:, :ON_VECTOR, :].rearrange("p (c i) t -> p c t i", i=4),
+            in_=z_low[:, :, :ON_VECTOR].rearrange("p t (c i) -> p c t i", i=4),
+        )
+        high3 = shared.tile([P, 2, 2, QUARTER], BF16, name="high3", offset=room, align_bytes=64)
         for d in range(2):
             gather_vector(d, 3, 1, high3[:, :, d, :])
-        z_b[0] = shared.tile([P, HALF, PACK], BF16, name="z_b0", offset=T * column, align_bytes=64)
         nc.gpsimd.tensor_scalar(
-            out=z_b[0][:, :ON_GPSIMD, :],
-            in0=z_low[:, :, :ON_GPSIMD].rearrange("p t c -> p c t"),
+            out=z_b[0][:, ON_VECTOR:, :],
+            in0=z_low[:, :, ON_VECTOR:].rearrange("p t c -> p c t"),
             scalar1=1.0,
             scalar2=0.0,
             op0=ALU.mult,
             op1=ALU.add,
         )
-        nc.vector.tensor_copy(
-            out=z_b[0][:, ON_GPSIMD:, :].rearrange("p (c i) t -> p c t i", i=4),
-            in_=z_low[:, :, ON_GPSIMD:].rearrange("p t (c i) -> p c t i", i=4),
-        )
         neighbours(*spans[0])
 
-        z_high = shared.tile([P, 2, PACK, QUARTER], BF16, name="z_high", offset=T * column, align_bytes=64)
-        largest(z_high[:, :, 1, :], high1[:, :, 0, :], high1[:, :, 1, :])
+        z_high = shared.tile([P, 2, PACK, QUARTER], BF16, name="z_high", offset=0, align_bytes=64)
         largest(z_high[:, :, 3, :], high3[:, :, 0, :], high3[:, :, 1, :])
 
         def piece(c0, c1):
             return c0 // QUARTER - 2, slice(c0 % QUARTER, (c1 - 1) % QUARTER + 1)
 
-        def largest_even(c0, c1):
+        def largest_rest(c0, c1):
             q, cols = piece(c0, c1)
-            largest(z_high[:, q, 0:PACK:2, cols], high_even[:, q, 0, :, cols], high_even[:, q, 1, :, cols])
+            largest(z_high[:, q, 0:3, cols], high[:, q, 0, :, cols], high[:, q, 1, :, cols])
 
-        def interleave_high(copy, c0, c1):
+        def interleave_high(copy, c0, c1, tag):
             q, cols = piece(c0, c1)
-            interleave(copy, z_high[:, q, :, cols], c0, c1)
+            interleave(copy, z_high[:, q, :, cols], c0, c1, tag)
 
-        largest_even(*spans[1])
-        largest_even(*spans[2])
-        interleave_high(nc.vector.tensor_copy, *spans[1])
-        interleave_high(nc.scalar.copy, *spans[2])
-        largest_even(*spans[3])
+        largest_rest(*spans[1])
+        largest_rest(*spans[2])
+        interleave_high(nc.vector.tensor_copy, *spans[1], "z_b1")
+        store(*spans[0])
+        interleave_high(nc.scalar.copy, *spans[2], "z_q0")
+        largest_rest(*spans[3])
         neighbours(*spans[1])
-        interleave_high(nc.vector.tensor_copy, *spans[3])
+        interleave_high(nc.vector.tensor_copy, *spans[3], "z_b3")
         neighbours(*spans[2])
         neighbours(*spans[3])
-        for span in spans:
+        for span in spans[1:]:
             store(*span)

@@ -117,9 +117,10 @@ def tile_picked_wsagecat_maxrelu_l_kernel(
         for c0 in range(0, T, QUARTER):
             first_layer(1, c0, QUARTER, c0 % HALF == 0)
         nc.sync.dma_start(out=copies[1][:], in_=plane(1))
-        for c0 in (0, HALF):
+        stretches = ((0, QUARTER), (QUARTER, HALF), (HALF, T))
+        for c0, c1 in stretches:
             for t in (2, 3, 0):
-                first_layer(t, c0, HALF, False)
+                first_layer(t, c0, c1 - c0, False)
         nc.sync.dma_start(out=copies[2][:], in_=plane(2))
 
         w23 = keep.tile([P, 2 * N], U32, name="w23", tag="w1_raw", align_bytes=64)
@@ -136,10 +137,10 @@ def tile_picked_wsagecat_maxrelu_l_kernel(
             shared.tile([P, HALF, PACK], BF16, name=f"h_b{n}", offset=n * room, align_bytes=64)
             for n in range(2)
         ]
-        for n in range(2):
+        for c0, c1 in stretches:
             nc.gpsimd.tensor_scalar(
-                out=h_b[n][:],
-                in0=h[:].rearrange("p (t c) -> p c t", t=PACK)[:, n * HALF : (n + 1) * HALF, :],
+                out=h_b[c0 // HALF][:, c0 % HALF : (c1 - 1) % HALF + 1, :],
+                in0=h[:].rearrange("p (t c) -> p c t", t=PACK)[:, c0:c1, :],
                 scalar1=1.0,
                 scalar2=0.0,
                 op0=ALU.mult,
@@ -261,22 +262,21 @@ def tile_picked_wsagecat_maxrelu_l_kernel(
         def piece(c0, c1):
             return c0 // QUARTER - 2, slice(c0 % QUARTER, (c1 - 1) % QUARTER + 1)
 
-        def largest_rest(c0, c1):
-            q, cols = piece(c0, c1)
-            largest(z_high[:, q, 0:3, cols], high[:, q, 0, :, cols], high[:, q, 1, :, cols])
+        def largest_rest(q, t0, t1):
+            largest(z_high[:, q, t0:t1, :], high[:, q, 0, t0:t1, :], high[:, q, 1, t0:t1, :])
 
         def interleave_high(copy, c0, c1, tag):
             q, cols = piece(c0, c1)
             interleave(copy, z_high[:, q, :, cols], c0, c1, tag)
 
-        largest_rest(*spans[1])
-        largest_rest(*spans[2])
+        largest_rest(0, 0, 3)
+        largest_rest(1, 0, 2)
         interleave_high(nc.vector.tensor_copy, *spans[1], "z_b1")
-        store(*spans[0])
-        interleave_high(nc.scalar.copy, *spans[2], "z_q0")
-        largest_rest(*spans[3])
+        largest_rest(1, 2, 3)
         neighbours(*spans[1])
-        interleave_high(nc.vector.tensor_copy, *spans[3], "z_b3")
+        store(*spans[0])
+        interleave_high(nc.vector.tensor_copy, *spans[2], "z_b2")
+        interleave_high(nc.scalar.copy, *spans[3], "z_q0")
         neighbours(*spans[2])
         neighbours(*spans[3])
         for span in spans[1:]:

@@ -19,8 +19,7 @@ P = 128
 PACK = 4
 HALF = 512
 QUARTER = 256
-CHUNKS = (512, 256, 128, 128)
-ON_VECTOR = 96
+EIGHTH = 128
 
 
 def tile_picked_wsagecat_maxrelu_l_kernel(
@@ -29,7 +28,6 @@ def tile_picked_wsagecat_maxrelu_l_kernel(
     nc = tc.nc
     with ExitStack() as ctx:
         keep = ctx.enter_context(tc.tile_pool(name="keep", bufs=1))
-        shared = ctx.enter_context(tc.tile_pool(name="shared", bufs=1))
         psum = ctx.enter_context(tc.psum_pool(name="psum", bufs=1))
 
         def load_scales(tile, cols, src):
@@ -79,15 +77,15 @@ def tile_picked_wsagecat_maxrelu_l_kernel(
             )
 
         nc.vector.tensor_copy(out=w1_dst[:, : P // 2, :, :], in_=lo_src)
-        nc.vector.tensor_copy(out=w1_dst[:, P // 2 :, 1, :], in_=hi_src[:, :, 1, :])
+        nc.vector.tensor_copy(out=w1_dst[:, P // 2 :, 3, :], in_=hi_src[:, :, 3, :])
         nc.vector.tensor_copy(out=w1_dst[:, P // 2 :, 0, :], in_=hi_src[:, :, 0, :])
-        nc.scalar.activation(out=w1_dst[:, P // 2 :, 2:4, :], in_=hi_src[:, :, 2:4, :], func=ACT.Copy)
-        quant_w1(1, 2)
-        quant_w1(2, 4)
+        nc.scalar.activation(out=w1_dst[:, P // 2 :, 1:3, :], in_=hi_src[:, :, 1:3, :], func=ACT.Copy)
+        quant_w1(3, 4)
+        quant_w1(1, 3)
         quant_w1(0, 1)
 
         h = keep.tile([P, PACK * T], F32, name="h", align_bytes=64)
-        copies = {t: keep.tile([P, T], F32, name=f"plane{t}", align_bytes=64) for t in (1, 2)}
+        copies = {t: keep.tile([P, T], F32, name=f"plane{t}", align_bytes=64) for t in (1, 2, 3)}
 
         def plane(t):
             return h[:, t * T : (t + 1) * T]
@@ -115,13 +113,13 @@ def tile_picked_wsagecat_maxrelu_l_kernel(
                 nc.scalar.activation(out=dst, in_=acc[:, :width], func=ACT.Relu)
 
         for c0 in range(0, T, QUARTER):
-            first_layer(1, c0, QUARTER, c0 % HALF == 0)
-        nc.sync.dma_start(out=copies[1][:], in_=plane(1))
-        stretches = ((0, QUARTER), (QUARTER, HALF), (HALF, T))
-        for c0, c1 in stretches:
-            for t in (2, 3, 0):
+            first_layer(3, c0, QUARTER, c0 % HALF == 0)
+        nc.sync.dma_start(out=copies[3][:], in_=plane(3))
+        for c0, c1 in ((0, QUARTER), (QUARTER, HALF), (HALF, T)):
+            for t in (2, 1, 0):
                 first_layer(t, c0, c1 - c0, False)
-        nc.sync.dma_start(out=copies[2][:], in_=plane(2))
+        for t in (2, 1):
+            nc.sync.dma_start(out=copies[t][:], in_=plane(t))
 
         w23 = keep.tile([P, 2 * N], U32, name="w23", tag="w1_raw", align_bytes=64)
         w23_sc = keep.tile([P, 2 * N], U8, name="w23_sc", tag="w1_b", align_bytes=64)
@@ -131,54 +129,59 @@ def tile_picked_wsagecat_maxrelu_l_kernel(
         load_scales(w23_sc, slice(0, N), w2_scales)
         load_scales(w23_sc, slice(N, 2 * N), w3_scales)
 
-        column = PACK * 2
-        room = HALF * column
-        h_b = [
-            shared.tile([P, HALF, PACK], BF16, name=f"h_b{n}", offset=n * room, align_bytes=64)
-            for n in range(2)
-        ]
-        for c0, c1 in stretches:
-            nc.gpsimd.tensor_scalar(
-                out=h_b[c0 // HALF][:, c0 % HALF : (c1 - 1) % HALF + 1, :],
-                in0=h[:].rearrange("p (t c) -> p c t", t=PACK)[:, c0:c1, :],
-                scalar1=1.0,
-                scalar2=0.0,
-                op0=ALU.mult,
-                op1=ALU.add,
-            )
+        lead = 7 * EIGHTH
+        room = keep.tile([P, lead + PACK * T], BF16, name="room", align_bytes=64)
 
-        def gather_vector(d, t, n, dst):
-            nc.vector.tensor_copy(out=dst, in_=plane(t).indirect(lists[d][:, n * HALF // 16 : (n + 1) * HALF // 16]))
+        def bytes_at(start, count):
+            return room[:, start : start + count]
 
-        def gather_scalar(d, t, q, dst):
-            nc.scalar.activation(
-                out=dst,
-                in_=copies.get(t, h)[:].indirect(lists[d][:, q * QUARTER // 16 : (q + 1) * QUARTER // 16]),
-                func=ACT.Copy,
-            )
+        h_b = bytes_at(lead, PACK * T).rearrange("p (c t) -> p c t", t=PACK)
 
-        low = [keep.tile([P, 2, PACK, QUARTER], BF16, name=f"low{d}", align_bytes=64) for d in range(2)]
-        for t in (1, 2, 3):
+        def weave_gpsimd(dst, src):
+            nc.gpsimd.tensor_scalar(out=dst, in0=src, scalar1=1.0, scalar2=0.0, op0=ALU.mult, op1=ALU.add)
+
+        for c0, c1 in ((0, QUARTER), (QUARTER, HALF - 32), (HALF - 32, T)):
+            weave_gpsimd(h_b[:, c0:c1, :], h[:].rearrange("p (t c) -> p c t", t=PACK)[:, c0:c1, :])
+
+        def offsets(d, c0, c1):
+            return lists[d][:, c0 // 16 : c1 // 16]
+
+        pairs = keep.tile([P, 2, 3, QUARTER, 2], BF16, name="pairs", align_bytes=64)
+
+        def gather_vector(t, c0, c1):
             for d in range(2):
-                gather_vector(d, t, 0, low[d][:, :, t, :])
-        for q in range(2):
-            for d in range(2):
-                gather_scalar(d, 0, q, low[d][:, q, 0, :])
-        high = keep.tile([P, 2, 2, 3, QUARTER], BF16, name="high", align_bytes=64)
-        for q in range(2):
-            for t in range(3):
+                blocks = pairs[:, d, 1:3] if t >= 2 else pairs[:, d, 0:1]
+                nc.vector.tensor_copy(
+                    out=blocks.rearrange("p b c e -> p (b c) e")[:, :, t % 2],
+                    in_=plane(t).indirect(offsets(d, c0, c1)),
+                )
+
+        def gather_scalar(dst, order, c0, c1):
+            for t in order:
                 for d in range(2):
-                    gather_scalar(d, t, 2 + q, high[:, q, d, t, :])
+                    nc.scalar.activation(
+                        out=dst[:, d, t, :], in_=copies.get(t, h)[:].indirect(offsets(d, c0, c1)), func=ACT.Copy
+                    )
+
+        def planes_of(view, width):
+            return view.rearrange("p (d t c) -> p d t c", d=2, c=width)
+
+        for t in (3, 2):
+            gather_vector(t, HALF, T)
+        for t in (1, 0):
+            gather_vector(t, HALF, HALF + QUARTER)
+        got_a = keep.tile([P, 2, PACK, QUARTER], BF16, name="got_a", align_bytes=64)
+        gather_scalar(got_a, (0, 3, 2, 1), 0, QUARTER)
 
         h_q = keep.tile([P, T], U32, name="h_q", align_bytes=64)
         h_sc = keep.tile([P, T], U8, name="h_sc", align_bytes=64)
-        z_q = {}
+        z_q = keep.tile([P, T], U32, name="z_q", align_bytes=64)
         z_sc = keep.tile([P, T], U8, name="z_sc", align_bytes=64)
         res = keep.tile([P, T], F32, name="res", align_bytes=64)
 
         def quantize(codes, scales, values, c0, c1):
             nc.vector.quantize_mx(
-                out=codes.bitcast(FP8X4),
+                out=codes[:, c0:c1].bitcast(FP8X4),
                 scales=scales[:, c0:c1],
                 in_=values.rearrange("p c t -> p (c t)"),
             )
@@ -189,95 +192,82 @@ def tile_picked_wsagecat_maxrelu_l_kernel(
             first = c0 not in accs
             if first:
                 accs[c0] = psum.tile([P, HALF], F32, name="out_acc", tag=f"bank{(4 + len(accs)) % 8}")
-            codes_in = z_q[c0][:] if which else h_q[:, c0:c1]
-            scales_in = z_sc if which else h_sc
+            codes, scales = (z_q, z_sc) if which else (h_q, h_sc)
             nc.tensor.matmul_mx(
                 out=accs[c0][:, : c1 - c0],
                 lhsT=w23[:, which * N : (which + 1) * N].bitcast(FP8X4),
                 lhsT_scale=w23_sc[:, which * N : (which + 1) * N],
-                rhs=codes_in.bitcast(FP8X4),
-                rhs_scale=scales_in[:, c0:c1],
+                rhs=codes[:, c0:c1].bitcast(FP8X4),
+                rhs_scale=scales[:, c0:c1],
                 start=first,
                 stop=not first,
             )
 
-        edges = [sum(CHUNKS[:n]) for n in range(len(CHUNKS) + 1)]
-        spans = list(zip(edges[:-1], edges[1:]))
-        z_b = {}
+        span_a, span_c, span_d = (0, 256), (256, 384), (384, 512)
+        span_b, span_e = (512, 768), (768, 1024)
 
-        def own(c0):
-            quantize(h_q[:, c0 : c0 + HALF], h_sc, h_b[c0 // HALF][:], c0, c0 + HALF)
-            for s0, s1 in spans:
-                if c0 <= s0 < c0 + HALF:
-                    second_layer(s0, s1, 0)
+        for c0 in (0, HALF):
+            quantize(h_q, h_sc, h_b[:, c0 : c0 + HALF, :], c0, c0 + HALF)
+        for span in (span_b, span_a, span_e, span_c, span_d):
+            second_layer(*span, 0)
+
+        got_d = planes_of(bytes_at(lead, 2 * PACK * EIGHTH), EIGHTH)
+        got_c = planes_of(bytes_at(lead + 2 * PACK * EIGHTH, 2 * PACK * EIGHTH), EIGHTH)
+        gather_scalar(got_c, (3, 2, 1, 0), *span_c)
 
         def largest(dst, first, second):
             nc.vector.tensor_tensor(out=dst, in0=first, in1=second, op=ALU.max)
 
-        def interleave(copy, planes, c0, c1, tag):
-            z_b[c0] = keep.tile([P, c1 - c0, PACK], BF16, name=f"z_b{c0}", tag=tag, align_bytes=64)
-            copy(
-                out=z_b[c0][:].rearrange("p (c i) t -> p c t i", i=4),
-                in_=planes.rearrange("p t (c i) -> p c t i", i=4),
-            )
+        def largest_pairs(dst, step):
+            both = [pairs[:, d, 0 : step + 1 : step].rearrange("p u c e -> p c u e") for d in range(2)]
+            largest(dst.rearrange("p c (u e) -> p c u e", e=2), *both)
 
-        def neighbours(c0, c1):
-            z_q[c0] = keep.tile([P, c1 - c0], U32, name=f"z_q{c0}", tag=f"z_q{c0}", align_bytes=64)
-            quantize(z_q[c0][:], z_sc, z_b[c0][:], c0, c1)
+        def woven(view):
+            return view.rearrange("p (c t) -> p c t", t=PACK)
+
+        def neighbours(values, c0, c1):
+            quantize(z_q, z_sc, values, c0, c1)
             second_layer(c0, c1, 1)
 
-        def store(c0, c1):
-            if c1 < T:
-                nc.scalar.activation(out=res[:, c0:c1], in_=accs[c0][:, : c1 - c0], func=ACT.Relu)
-            else:
+        def store(c0, c1, on_vector):
+            if on_vector:
                 nc.vector.tensor_scalar_max(out=res[:, c0:c1], in0=accs[c0][:, : c1 - c0], scalar1=0.0)
+            else:
+                nc.scalar.activation(out=res[:, c0:c1], in_=accs[c0][:, : c1 - c0], func=ACT.Relu)
             nc.sync.dma_start(out=out[:, c0:c1], in_=res[:, c0:c1])
 
-        own(0)
-        own(HALF)
-        z_low = shared.tile([P, PACK, HALF], BF16, name="z_low", offset=0, align_bytes=64)
-        for q in range(2):
-            largest(z_low[:, :, q * QUARTER : (q + 1) * QUARTER], low[0][:, q, :, :], low[1][:, q, :, :])
-        z_b[0] = shared.tile([P, HALF, PACK], BF16, name="z_b0", offset=2 * room, align_bytes=64)
-        nc.vector.tensor_copy(
-            out=z_b[0][:, :ON_VECTOR, :].rearrange("p (c i) t -> p c t i", i=4),
-            in_=z_low[:, :, :ON_VECTOR].rearrange("p t (c i) -> p c t i", i=4),
-        )
-        high3 = shared.tile([P, 2, 2, QUARTER], BF16, name="high3", offset=room, align_bytes=64)
-        for d in range(2):
-            gather_vector(d, 3, 1, high3[:, :, d, :])
-        nc.gpsimd.tensor_scalar(
-            out=z_b[0][:, ON_VECTOR:, :],
-            in0=z_low[:, :, ON_VECTOR:].rearrange("p t c -> p c t"),
-            scalar1=1.0,
-            scalar2=0.0,
-            op0=ALU.mult,
-            op1=ALU.add,
-        )
-        neighbours(*spans[0])
-
-        z_high = shared.tile([P, 2, PACK, QUARTER], BF16, name="z_high", offset=0, align_bytes=64)
-        largest(z_high[:, :, 3, :], high3[:, :, 0, :], high3[:, :, 1, :])
-
-        def piece(c0, c1):
-            return c0 // QUARTER - 2, slice(c0 % QUARTER, (c1 - 1) % QUARTER + 1)
-
-        def largest_rest(q, t0, t1):
-            largest(z_high[:, q, t0:t1, :], high[:, q, 0, t0:t1, :], high[:, q, 1, t0:t1, :])
-
-        def interleave_high(copy, c0, c1, tag):
-            q, cols = piece(c0, c1)
-            interleave(copy, z_high[:, q, :, cols], c0, c1, tag)
-
-        largest_rest(0, 0, 3)
-        largest_rest(1, 0, 2)
-        interleave_high(nc.vector.tensor_copy, *spans[1], "z_b1")
-        largest_rest(1, 2, 3)
-        neighbours(*spans[1])
-        store(*spans[0])
-        interleave_high(nc.vector.tensor_copy, *spans[2], "z_b2")
-        interleave_high(nc.scalar.copy, *spans[3], "z_q0")
-        neighbours(*spans[2])
-        neighbours(*spans[3])
-        for span in spans[1:]:
-            store(*span)
+        upper = lead + PACK * HALF
+        z_b = woven(bytes_at(0, PACK * QUARTER))
+        largest_pairs(z_b, 1)
+        top_a = bytes_at(upper, PACK * QUARTER).rearrange("p (t c) -> p t c", t=PACK)
+        largest(top_a, got_a[:, 0], got_a[:, 1])
+        z_a = keep.tile([P, QUARTER, PACK], BF16, name="z_a", align_bytes=64)
+        weave_gpsimd(z_a[:], top_a.rearrange("p t c -> p c t"))
+        gather_vector(1, *span_e)
+        neighbours(z_b, *span_b)
+        gather_scalar(got_d, (3, 2, 1, 0), *span_d)
+        top_c = keep.tile([P, PACK, EIGHTH], BF16, name="top_c", align_bytes=64)
+        largest(top_c[:], got_c[:, 0], got_c[:, 1])
+        z_c = keep.tile([P, EIGHTH, PACK], BF16, name="z_c", align_bytes=64)
+        weave_gpsimd(z_c[:], top_c[:].rearrange("p t c -> p c t"))
+        gather_vector(0, *span_e)
+        neighbours(z_a[:], *span_a)
+        z_e = woven(bytes_at(upper + PACK * EIGHTH, PACK * QUARTER))
+        largest_pairs(z_e, 2)
+        top_d = bytes_at(upper, PACK * EIGHTH).rearrange("p (t c) -> p t c", t=PACK)
+        largest(top_d, got_d[:, 0], got_d[:, 1])
+        store(*span_b, False)
+        store(*span_a, False)
+        neighbours(z_e, *span_e)
+        z_d = keep.tile([P, EIGHTH, PACK], BF16, name="z_d", align_bytes=64)
+        for copy, c0 in ((nc.vector.tensor_copy, 0), (nc.scalar.copy, EIGHTH // 2)):
+            cols = slice(c0, c0 + EIGHTH // 2)
+            copy(
+                out=z_d[:, cols, :].rearrange("p (c i) t -> p c t i", i=4),
+                in_=top_d[:, :, cols].rearrange("p t (c i) -> p c t i", i=4),
+            )
+        neighbours(z_c[:], *span_c)
+        neighbours(z_d[:], *span_d)
+        store(*span_e, False)
+        store(*span_c, False)
+        store(*span_d, True)

@@ -20,6 +20,7 @@ PACK = 4
 HALF = 512
 QUARTER = 256
 EIGHTH = 128
+SPLIT = 480
 
 
 def tile_picked_wsagecat_maxrelu_l_kernel(
@@ -129,32 +130,39 @@ def tile_picked_wsagecat_maxrelu_l_kernel(
         load_scales(w23_sc, slice(0, N), w2_scales)
         load_scales(w23_sc, slice(N, 2 * N), w3_scales)
 
-        lead = 7 * EIGHTH
-        room = keep.tile([P, lead + PACK * T], BF16, name="room", align_bytes=64)
+        room = keep.tile([P, 11200], BF16, name="room", align_bytes=64)
 
         def bytes_at(start, count):
             return room[:, start : start + count]
 
-        h_b = bytes_at(lead, PACK * T).rearrange("p (c t) -> p c t", t=PACK)
+        def woven(view):
+            return view.rearrange("p (c t) -> p c t", t=PACK)
+
+        def by_plane(view):
+            return view.rearrange("p (t c) -> p t c", t=PACK)
+
+        lead = 3840
+        h_b = woven(bytes_at(lead, PACK * T))
 
         def weave_gpsimd(dst, src):
             nc.gpsimd.tensor_scalar(out=dst, in0=src, scalar1=1.0, scalar2=0.0, op0=ALU.mult, op1=ALU.add)
 
-        for c0, c1 in ((0, QUARTER), (QUARTER, HALF - 32), (HALF - 32, T)):
+        for c0, c1 in ((0, QUARTER), (QUARTER, HALF - 4), (HALF - 4, T)):
             weave_gpsimd(h_b[:, c0:c1, :], h[:].rearrange("p (t c) -> p c t", t=PACK)[:, c0:c1, :])
 
         def offsets(d, c0, c1):
             return lists[d][:, c0 // 16 : c1 // 16]
 
-        pairs = keep.tile([P, 2, 3, QUARTER, 2], BF16, name="pairs", align_bytes=64)
+        wide = T - SPLIT
+        low_at = (9024, lead + PACK * HALF)
+        high_at = (10112, 7936)
 
-        def gather_vector(t, c0, c1):
-            for d in range(2):
-                blocks = pairs[:, d, 1:3] if t >= 2 else pairs[:, d, 0:1]
-                nc.vector.tensor_copy(
-                    out=blocks.rearrange("p b c e -> p (b c) e")[:, :, t % 2],
-                    in_=plane(t).indirect(offsets(d, c0, c1)),
-                )
+        def gather_vector(d, t):
+            start = high_at[d] if t >= 2 else low_at[d]
+            nc.vector.tensor_copy(
+                out=bytes_at(start, 2 * wide).rearrange("p (c e) -> p c e", e=2)[:, :, t % 2],
+                in_=plane(t).indirect(offsets(d, SPLIT, T)),
+            )
 
         def gather_scalar(dst, order, c0, c1):
             for t in order:
@@ -163,13 +171,8 @@ def tile_picked_wsagecat_maxrelu_l_kernel(
                         out=dst[:, d, t, :], in_=copies.get(t, h)[:].indirect(offsets(d, c0, c1)), func=ACT.Copy
                     )
 
-        def planes_of(view, width):
-            return view.rearrange("p (d t c) -> p d t c", d=2, c=width)
-
-        for t in (3, 2):
-            gather_vector(t, HALF, T)
-        for t in (1, 0):
-            gather_vector(t, HALF, HALF + QUARTER)
+        for d, t in ((0, 3), (1, 3), (0, 2), (1, 2), (0, 1), (0, 0)):
+            gather_vector(d, t)
         got_a = keep.tile([P, 2, PACK, QUARTER], BF16, name="got_a", align_bytes=64)
         gather_scalar(got_a, (0, 3, 2, 1), 0, QUARTER)
 
@@ -204,30 +207,19 @@ def tile_picked_wsagecat_maxrelu_l_kernel(
             )
 
         span_a, span_c, span_d = (0, 256), (256, 384), (384, 512)
-        span_b, span_e = (512, 768), (768, 1024)
+        span_e, span_f = (512, 768), (768, 1024)
 
         for c0 in (0, HALF):
             quantize(h_q, h_sc, h_b[:, c0 : c0 + HALF, :], c0, c0 + HALF)
-        for span in (span_b, span_a, span_e, span_c, span_d):
+        for span in (span_a, span_e, span_f, span_c, span_d):
             second_layer(*span, 0)
 
-        got_d = planes_of(bytes_at(lead, 2 * PACK * EIGHTH), EIGHTH)
-        got_c = planes_of(bytes_at(lead + 2 * PACK * EIGHTH, 2 * PACK * EIGHTH), EIGHTH)
-        gather_scalar(got_c, (3, 2, 1, 0), *span_c)
+        rest = SPLIT - QUARTER
+        got_d = bytes_at(lead + QUARTER, 2 * PACK * rest).rearrange("p (d t c) -> p d t c", d=2, c=rest)
+        gather_scalar(got_d, (3, 2, 1, 0), QUARTER, SPLIT)
 
         def largest(dst, first, second):
             nc.vector.tensor_tensor(out=dst, in0=first, in1=second, op=ALU.max)
-
-        def largest_pairs(dst, step):
-            both = [pairs[:, d, 0 : step + 1 : step].rearrange("p u c e -> p c u e") for d in range(2)]
-            largest(dst.rearrange("p c (u e) -> p c u e", e=2), *both)
-
-        def woven(view):
-            return view.rearrange("p (c t) -> p c t", t=PACK)
-
-        def neighbours(values, c0, c1):
-            quantize(z_q, z_sc, values, c0, c1)
-            second_layer(c0, c1, 1)
 
         def store(c0, c1, on_vector):
             if on_vector:
@@ -236,38 +228,42 @@ def tile_picked_wsagecat_maxrelu_l_kernel(
                 nc.scalar.activation(out=res[:, c0:c1], in_=accs[c0][:, : c1 - c0], func=ACT.Relu)
             nc.sync.dma_start(out=out[:, c0:c1], in_=res[:, c0:c1])
 
-        upper = lead + PACK * HALF
-        z_b = woven(bytes_at(0, PACK * QUARTER))
-        largest_pairs(z_b, 1)
-        top_a = bytes_at(upper, PACK * QUARTER).rearrange("p (t c) -> p t c", t=PACK)
+        def neighbours(values, c0, c1):
+            quantize(z_q, z_sc, values, c0, c1)
+            second_layer(c0, c1, 1)
+
+        top_a = by_plane(bytes_at(lead - 3 * QUARTER, PACK * QUARTER))
         largest(top_a, got_a[:, 0], got_a[:, 1])
         z_a = keep.tile([P, QUARTER, PACK], BF16, name="z_a", align_bytes=64)
         weave_gpsimd(z_a[:], top_a.rearrange("p t c -> p c t"))
-        gather_vector(1, *span_e)
-        neighbours(z_b, *span_b)
-        gather_scalar(got_d, (3, 2, 1, 0), *span_d)
-        top_c = keep.tile([P, PACK, EIGHTH], BF16, name="top_c", align_bytes=64)
-        largest(top_c[:], got_c[:, 0], got_c[:, 1])
-        z_c = keep.tile([P, EIGHTH, PACK], BF16, name="z_c", align_bytes=64)
-        weave_gpsimd(z_c[:], top_c[:].rearrange("p t c -> p c t"))
-        gather_vector(0, *span_e)
+        for t in (1, 0):
+            gather_vector(1, t)
         neighbours(z_a[:], *span_a)
-        z_e = woven(bytes_at(upper + PACK * EIGHTH, PACK * QUARTER))
-        largest_pairs(z_e, 2)
-        top_d = bytes_at(upper, PACK * EIGHTH).rearrange("p (t c) -> p t c", t=PACK)
+        z_rest = woven(bytes_at(64, PACK * (T - QUARTER)))
+
+        def z_cols(c0, c1):
+            return z_rest[:, c0 - QUARTER : c1 - QUARTER, :]
+
+        both = []
+        for d in range(2):
+            step = high_at[d] - low_at[d]
+            halves = bytes_at(low_at[d], 2 * step).rearrange("p (u x) -> p u x", u=2)[:, :, : 2 * wide]
+            both.append(halves.rearrange("p u (c e) -> p c u e", e=2))
+        largest(z_cols(SPLIT, T).rearrange("p c (u e) -> p c u e", e=2), *both)
+        top_d = by_plane(bytes_at(lead + QUARTER - PACK * rest, PACK * rest))
         largest(top_d, got_d[:, 0], got_d[:, 1])
-        store(*span_b, False)
         store(*span_a, False)
-        neighbours(z_e, *span_e)
-        z_d = keep.tile([P, EIGHTH, PACK], BF16, name="z_d", align_bytes=64)
-        for copy, c0 in ((nc.vector.tensor_copy, 0), (nc.scalar.copy, EIGHTH // 2)):
-            cols = slice(c0, c0 + EIGHTH // 2)
+        quantize(z_q, z_sc, z_cols(HALF, T), HALF, T)
+        second_layer(*span_e, 1)
+        second_layer(*span_f, 1)
+        for copy, c0, c1 in ((nc.scalar.copy, *span_c), (nc.vector.tensor_copy, span_d[0], SPLIT)):
             copy(
-                out=z_d[:, cols, :].rearrange("p (c i) t -> p c t i", i=4),
-                in_=top_d[:, :, cols].rearrange("p t (c i) -> p c t i", i=4),
+                out=z_cols(c0, c1).rearrange("p (c i) t -> p c t i", i=4),
+                in_=top_d[:, :, c0 - QUARTER : c1 - QUARTER].rearrange("p t (c i) -> p c t i", i=4),
             )
-        neighbours(z_c[:], *span_c)
-        neighbours(z_d[:], *span_d)
-        store(*span_e, False)
-        store(*span_c, False)
-        store(*span_d, True)
+        for span in (span_c, span_d):
+            neighbours(z_cols(*span), *span)
+        for span in (span_e, span_f):
+            store(*span, False)
+        for span in (span_c, span_d):
+            store(*span, True)

@@ -43,17 +43,18 @@ def tile_picked_wsagecat_maxrelu_l_kernel(
 
         x_sc = keep.tile([P, QUARTER], U8, name="x_sc", align_bytes=64)
         nc.vector.memset(x_sc[:].bitcast(U32), 0)
-        w1_raw = keep.tile([P, PACK, H // 2], F32, name="w1_raw", tag="w1_raw", align_bytes=64)
-        w1_hi = keep.tile([P, PACK, H // 2], F32, name="w1_hi", align_bytes=64)
         w1_rows = w1.rearrange("(p j) c -> p j c", j=PACK)
-        nc.sync.dma_start(out=w1_raw[:], in_=w1_rows[:, :, : H // 2])
-        nc.sync.dma_start(out=w1_hi[:], in_=w1_rows[:, :, H // 2 :])
+        w1_parts = []
+        for n, (c0, c1) in enumerate(((0, 256), (256, 384), (384, 512))):
+            part = keep.tile([P, PACK, c1 - c0], F32, name=f"w1_raw{n}", tag=f"w1_raw{n}", align_bytes=64)
+            nc.sync.dma_start(out=part[:], in_=w1_rows[:, :, c0:c1])
+            w1_parts.append((slice(c0 // PACK, c1 // PACK), part[:].rearrange("p j (m t) -> p m t j", t=PACK)))
         for q in range(4):
             nc.sync.dma_start(
                 out=x_sc[32 * q : 32 * q + 16, :].bitcast(I32),
                 in_=x_scales[0, 4 * q : 4 * q + 4, :].bitcast(I32).rearrange("r (a c) -> a r c", a=4),
             )
-        x_w = keep.tile([P, T], U32, name="x_w", align_bytes=64)
+        x_w = keep.tile([P, T], U32, name="x_w", tag="x_w", align_bytes=64)
         x_src = x_words[0].rearrange("p n t -> p (n t)").bitcast(I32)
         for c0 in (0, HALF):
             nc.sync.dma_start(out=x_w[:, c0 : c0 + HALF].bitcast(I32), in_=x_src[:, c0 : c0 + HALF])
@@ -66,24 +67,25 @@ def tile_picked_wsagecat_maxrelu_l_kernel(
         w1_b = keep.tile([P, PACK, P, PACK], BF16, name="w1_b", tag="w1_b", align_bytes=64)
         w1_q = keep.tile([P, H], U32, name="w1_q", align_bytes=64)
         w1_sc = keep.tile([P, H], U8, name="w1_sc", align_bytes=64)
-        lo_src = w1_raw[:].rearrange("p j (m t) -> p m t j", t=PACK)
-        hi_src = w1_hi[:].rearrange("p j (m t) -> p m t j", t=PACK)
         w1_dst = w1_b[:].rearrange("p t m j -> p m t j")
 
-        def quant_w1(t0, t1):
+        def quant_w1(c0, c1):
             nc.vector.quantize_mx(
-                out=w1_q[:, t0 * P : t1 * P].bitcast(FP8X4),
-                scales=w1_sc[:, t0 * P : t1 * P],
-                in_=w1_b[:, t0:t1, :, :].rearrange("p t m j -> p (t m j)"),
+                out=w1_q[:, c0:c1].bitcast(FP8X4),
+                scales=w1_sc[:, c0:c1],
+                in_=w1_b[:].rearrange("p t m j -> p (t m j)")[:, PACK * c0 : PACK * c1],
             )
 
-        nc.vector.tensor_copy(out=w1_dst[:, : P // 2, :, :], in_=lo_src)
-        nc.vector.tensor_copy(out=w1_dst[:, P // 2 :, 3, :], in_=hi_src[:, :, 3, :])
-        nc.vector.tensor_copy(out=w1_dst[:, P // 2 :, 0, :], in_=hi_src[:, :, 0, :])
-        nc.scalar.activation(out=w1_dst[:, P // 2 :, 1:3, :], in_=hi_src[:, :, 1:3, :], func=ACT.Copy)
-        quant_w1(3, 4)
-        quant_w1(1, 3)
-        quant_w1(0, 1)
+        for rows, part in w1_parts[:2]:
+            nc.vector.tensor_copy(out=w1_dst[:, rows, :, :], in_=part)
+        quant_w1(3 * P, 3 * P + P // 2)
+        rows, part = w1_parts[2]
+        nc.vector.tensor_copy(out=w1_dst[:, rows, 3, :], in_=part[:, :, 3, :])
+        nc.vector.tensor_copy(out=w1_dst[:, rows, 0, :], in_=part[:, :, 0, :])
+        nc.scalar.activation(out=w1_dst[:, rows, 1:3, :], in_=part[:, :, 1:3, :], func=ACT.Copy)
+        quant_w1(3 * P + P // 2, H)
+        quant_w1(P, 3 * P)
+        quant_w1(0, P)
 
         h = keep.tile([P, PACK * T], F32, name="h", align_bytes=64)
         copies = {t: keep.tile([P, T], F32, name=f"plane{t}", align_bytes=64) for t in (1, 2, 3)}
@@ -113,16 +115,20 @@ def tile_picked_wsagecat_maxrelu_l_kernel(
             else:
                 nc.scalar.activation(out=dst, in_=acc[:, :width], func=ACT.Relu)
 
+        def copy_half(t, c0):
+            nc.sync.dma_start(out=copies[t][:, c0 : c0 + HALF], in_=plane(t)[:, c0 : c0 + HALF])
+
         for c0 in range(0, T, QUARTER):
             first_layer(3, c0, QUARTER, c0 % HALF == 0)
-        nc.sync.dma_start(out=copies[3][:], in_=plane(3))
+            if c0 % HALF:
+                copy_half(3, c0 - QUARTER)
         for c0, c1 in ((0, QUARTER), (QUARTER, HALF), (HALF, T)):
             for t in (2, 1, 0):
                 first_layer(t, c0, c1 - c0, False)
-        for t in (2, 1):
-            nc.sync.dma_start(out=copies[t][:], in_=plane(t))
+                if t and c1 % HALF == 0:
+                    copy_half(t, c1 - HALF)
 
-        w23 = keep.tile([P, 2 * N], U32, name="w23", tag="w1_raw", align_bytes=64)
+        w23 = keep.tile([P, 2 * N], U32, name="w23", tag="w1_raw0", align_bytes=64)
         w23_sc = keep.tile([P, 2 * N], U8, name="w23_sc", tag="w1_b", align_bytes=64)
         nc.gpsimd.memset(w23_sc[:].bitcast(U32), 0)
         load_words(w23[:, 0:N], w2_words)
@@ -173,8 +179,8 @@ def tile_picked_wsagecat_maxrelu_l_kernel(
 
         for d, t in ((0, 3), (1, 3), (0, 2), (1, 2), (0, 1), (0, 0)):
             gather_vector(d, t)
-        got_a = keep.tile([P, 2, PACK, QUARTER], BF16, name="got_a", align_bytes=64)
-        gather_scalar(got_a, (0, 3, 2, 1), 0, QUARTER)
+        got_a = keep.tile([P, 2, PACK, QUARTER], BF16, name="got_a", tag="x_w", align_bytes=64)
+        gather_scalar(got_a, (3, 0, 2, 1), 0, QUARTER)
 
         h_q = keep.tile([P, T], U32, name="h_q", align_bytes=64)
         h_sc = keep.tile([P, T], U8, name="h_sc", align_bytes=64)
@@ -263,7 +269,5 @@ def tile_picked_wsagecat_maxrelu_l_kernel(
             )
         for span in (span_c, span_d):
             neighbours(z_cols(*span), *span)
-        for span in (span_e, span_f):
-            store(*span, False)
-        for span in (span_c, span_d):
-            store(*span, True)
+        for span, on_vector in ((span_e, False), (span_f, True), (span_c, False), (span_d, True)):
+            store(*span, on_vector)

@@ -128,11 +128,10 @@ def tile_picked_wsagecat_maxrelu_l_kernel(
                 if t and c1 % HALF == 0:
                     copy_half(t, c1 - HALF)
 
-        w23 = keep.tile([P, 2 * N], U32, name="w23", tag="w1_raw0", align_bytes=64)
+        w3_w = keep.tile([P, N], U32, name="w3_w", tag="w1_raw0", align_bytes=64)
         w23_sc = keep.tile([P, 2 * N], U8, name="w23_sc", tag="w1_b", align_bytes=64)
         nc.gpsimd.memset(w23_sc[:].bitcast(U32), 0)
-        load_words(w23[:, 0:N], w2_words)
-        load_words(w23[:, N : 2 * N], w3_words)
+        load_words(w3_w[:], w3_words)
         load_scales(w23_sc, slice(0, N), w2_scales)
         load_scales(w23_sc, slice(N, 2 * N), w3_scales)
 
@@ -196,6 +195,7 @@ def tile_picked_wsagecat_maxrelu_l_kernel(
             )
 
         accs = {}
+        weights = {1: w3_w}
 
         def second_layer(c0, c1, which):
             first = c0 not in accs
@@ -204,7 +204,7 @@ def tile_picked_wsagecat_maxrelu_l_kernel(
             codes, scales = (z_q, z_sc) if which else (h_q, h_sc)
             nc.tensor.matmul_mx(
                 out=accs[c0][:, : c1 - c0],
-                lhsT=w23[:, which * N : (which + 1) * N].bitcast(FP8X4),
+                lhsT=weights[which][:].bitcast(FP8X4),
                 lhsT_scale=w23_sc[:, which * N : (which + 1) * N],
                 rhs=codes[:, c0:c1].bitcast(FP8X4),
                 rhs_scale=scales[:, c0:c1],
@@ -217,8 +217,6 @@ def tile_picked_wsagecat_maxrelu_l_kernel(
 
         for c0 in (0, HALF):
             quantize(h_q, h_sc, h_b[:, c0 : c0 + HALF, :], c0, c0 + HALF)
-        for span in (span_a, span_e, span_f, span_c, span_d):
-            second_layer(*span, 0)
 
         rest = SPLIT - QUARTER
         got_d = bytes_at(lead + QUARTER, 2 * PACK * rest).rearrange("p (d t c) -> p d t c", d=2, c=rest)
@@ -240,6 +238,10 @@ def tile_picked_wsagecat_maxrelu_l_kernel(
 
         top_a = by_plane(bytes_at(lead - 3 * QUARTER, PACK * QUARTER))
         largest(top_a, got_a[:, 0], got_a[:, 1])
+        weights[0] = keep.tile([P, N], U32, name="w2_w", tag="x_w", align_bytes=64)
+        load_words(weights[0][:], w2_words)
+        for span in (span_a, span_e, span_f, span_c, span_d):
+            second_layer(*span, 0)
         z_a = keep.tile([P, QUARTER, PACK], BF16, name="z_a", align_bytes=64)
         weave_gpsimd(z_a[:], top_a.rearrange("p t c -> p c t"))
         for t in (1, 0):

@@ -261,9 +261,8 @@ def tile_picked_wsagecat_maxrelu_l_kernel(
         top_d = by_plane(bytes_at(lead + QUARTER - PACK * rest, PACK * rest))
         largest(top_d, got_d[:, 0], got_d[:, 1])
         store(*span_a, False)
-        quantize(z_q, z_sc, z_cols(HALF, T), HALF, T)
-        second_layer(*span_e, 1)
-        second_layer(*span_f, 1)
+        for span in (span_e, span_f):
+            neighbours(z_cols(*span), *span)
         for copy, c0, c1 in ((nc.scalar.copy, *span_c), (nc.vector.tensor_copy, span_d[0], SPLIT)):
             copy(
                 out=z_cols(c0, c1).rearrange("p (c i) t -> p c t i", i=4),
@@ -271,5 +270,5 @@ def tile_picked_wsagecat_maxrelu_l_kernel(
             )
         for span in (span_c, span_d):
             neighbours(z_cols(*span), *span)
-        for span, on_vector in ((span_e, False), (span_f, True), (span_c, False), (span_d, True)):
+        for span, on_vector in ((span_e, False), (span_f, False), (span_c, True), (span_d, True)):
             store(*span, on_vector)

@@ -20,7 +20,7 @@ PACK = 4
 HALF = 512
 QUARTER = 256
 EIGHTH = 128
-SPLIT = 480
+SPLIT = 512
 
 
 def tile_picked_wsagecat_maxrelu_l_kernel(
@@ -135,7 +135,7 @@ def tile_picked_wsagecat_maxrelu_l_kernel(
         load_scales(w23_sc, slice(0, N), w2_scales)
         load_scales(w23_sc, slice(N, 2 * N), w3_scales)
 
-        room = keep.tile([P, 11200], BF16, name="room", align_bytes=64)
+        room = keep.tile([P, 10752], BF16, name="room", align_bytes=64)
 
         def bytes_at(start, count):
             return room[:, start : start + count]
@@ -146,7 +146,7 @@ def tile_picked_wsagecat_maxrelu_l_kernel(
         def by_plane(view):
             return view.rearrange("p (t c) -> p t c", t=PACK)
 
-        lead = 3840
+        lead = 3584
         h_b = woven(bytes_at(lead, PACK * T))
 
         def weave_gpsimd(dst, src):
@@ -159,8 +159,8 @@ def tile_picked_wsagecat_maxrelu_l_kernel(
             return lists[d][:, c0 // 16 : c1 // 16]
 
         wide = T - SPLIT
-        low_at = (9024, lead + PACK * HALF)
-        high_at = (10112, 7936)
+        low_at = (8704, 5760)
+        high_at = (9728, 7680)
 
         def gather_vector(d, t):
             start = high_at[d] if t >= 2 else low_at[d]
@@ -219,7 +219,7 @@ def tile_picked_wsagecat_maxrelu_l_kernel(
             quantize(h_q, h_sc, h_b[:, c0 : c0 + HALF, :], c0, c0 + HALF)
 
         rest = SPLIT - QUARTER
-        got_d = bytes_at(lead + QUARTER, 2 * PACK * rest).rearrange("p (d t c) -> p d t c", d=2, c=rest)
+        got_d = bytes_at(lead + EIGHTH, 2 * PACK * rest).rearrange("p (d t c) -> p d t c", d=2, c=rest)
         gather_scalar(got_d, (3, 2, 1, 0), QUARTER, SPLIT)
 
         def largest(dst, first, second):
@@ -236,7 +236,7 @@ def tile_picked_wsagecat_maxrelu_l_kernel(
             quantize(z_q, z_sc, values, c0, c1)
             second_layer(c0, c1, 1)
 
-        top_a = by_plane(bytes_at(lead - 3 * QUARTER, PACK * QUARTER))
+        top_a = by_plane(bytes_at(1920, PACK * HALF))[:, :, :QUARTER]
         largest(top_a, got_a[:, 0], got_a[:, 1])
         weights[0] = keep.tile([P, N], U32, name="w2_w", tag="x_w", align_bytes=64)
         load_words(weights[0][:], w2_words)
@@ -247,10 +247,11 @@ def tile_picked_wsagecat_maxrelu_l_kernel(
         for t in (1, 0):
             gather_vector(1, t)
         neighbours(z_a[:], *span_a)
-        z_rest = woven(bytes_at(64, PACK * (T - QUARTER)))
+        z_high = woven(bytes_at(0, PACK * HALF))
+        z_d = keep.tile([P, QUARTER, PACK], BF16, name="z_d", align_bytes=64)
 
         def z_cols(c0, c1):
-            return z_rest[:, c0 - QUARTER : c1 - QUARTER, :]
+            return z_high[:, c0 - HALF : c1 - HALF, :] if c0 >= HALF else z_d[:, c0 - QUARTER : c1 - QUARTER, :]
 
         both = []
         for d in range(2):
@@ -258,8 +259,9 @@ def tile_picked_wsagecat_maxrelu_l_kernel(
             halves = bytes_at(low_at[d], 2 * step).rearrange("p (u x) -> p u x", u=2)[:, :, : 2 * wide]
             both.append(halves.rearrange("p u (c e) -> p c u e", e=2))
         largest(z_cols(SPLIT, T).rearrange("p c (u e) -> p c u e", e=2), *both)
-        top_d = by_plane(bytes_at(lead + QUARTER - PACK * rest, PACK * rest))
-        largest(top_d, got_d[:, 0], got_d[:, 1])
+        top_d = by_plane(bytes_at(PACK * HALF, PACK * rest))
+        for planes in (slice(1, PACK), slice(0, 1)):
+            largest(top_d[:, planes], got_d[:, 0, planes], got_d[:, 1, planes])
         store(*span_a, False)
         for span in (span_e, span_f):
             neighbours(z_cols(*span), *span)

@@ -260,17 +260,17 @@ def tile_picked_wsagecat_maxrelu_l_kernel(
             both.append(halves.rearrange("p u (c e) -> p c u e", e=2))
         largest(z_cols(SPLIT, T).rearrange("p c (u e) -> p c u e", e=2), *both)
         top_d = by_plane(bytes_at(PACK * HALF, PACK * rest))
-        for planes in (slice(1, PACK), slice(0, 1)):
-            largest(top_d[:, planes], got_d[:, 0, planes], got_d[:, 1, planes])
+        largest(top_d[:, 1:], got_d[:, 0, 1:], got_d[:, 1, 1:])
+        neighbours(z_cols(*span_e), *span_e)
+        largest(top_d[:, 0], got_d[:, 0, 0], got_d[:, 1, 0])
         store(*span_a, False)
-        for span in (span_e, span_f):
-            neighbours(z_cols(*span), *span)
-        for copy, c0, c1 in ((nc.scalar.copy, *span_c), (nc.vector.tensor_copy, span_d[0], SPLIT)):
+        neighbours(z_cols(*span_f), *span_f)
+        for copy, c0, c1 in ((nc.scalar.copy, *span_c), (nc.vector.tensor_copy, *span_d)):
             copy(
                 out=z_cols(c0, c1).rearrange("p (c i) t -> p c t i", i=4),
                 in_=top_d[:, :, c0 - QUARTER : c1 - QUARTER].rearrange("p t (c i) -> p c t i", i=4),
             )
-        for span in (span_c, span_d):
+        for span in (span_d, span_c):
             neighbours(z_cols(*span), *span)
-        for span, on_vector in ((span_e, False), (span_f, False), (span_c, True), (span_d, True)):
+        for span, on_vector in ((span_e, False), (span_f, False), (span_d, True), (span_c, True)):
             store(*span, on_vector)

@@ -124,16 +124,16 @@ def tile_picked_wsagecat_maxrelu_l_kernel(
                 copy_half(3, c0 - QUARTER)
         for c0, c1 in ((0, QUARTER), (QUARTER, HALF), (HALF, T)):
             for t in (2, 1, 0):
-                first_layer(t, c0, c1 - c0, False)
+                first_layer(t, c0, c1 - c0, (t, c0) == (2, 0))
                 if t and c1 % HALF == 0:
                     copy_half(t, c1 - HALF)
 
         w3_w = keep.tile([P, N], U32, name="w3_w", tag="w1_raw0", align_bytes=64)
-        w23_sc = keep.tile([P, 2 * N], U8, name="w23_sc", tag="w1_b", align_bytes=64)
-        nc.gpsimd.memset(w23_sc[:].bitcast(U32), 0)
+        w2_sc = keep.tile([P, N], U8, name="w2_sc", tag="w1_b", align_bytes=64)
+        nc.gpsimd.memset(w2_sc[:].bitcast(U32), 0)
         load_words(w3_w[:], w3_words)
-        load_scales(w23_sc, slice(0, N), w2_scales)
-        load_scales(w23_sc, slice(N, 2 * N), w3_scales)
+        load_scales(w2_sc, slice(0, N), w2_scales)
+        load_scales(x_sc, slice(0, N), w3_scales)
 
         room = keep.tile([P, 10752], BF16, name="room", align_bytes=64)
 
@@ -205,7 +205,7 @@ def tile_picked_wsagecat_maxrelu_l_kernel(
             nc.tensor.matmul_mx(
                 out=accs[c0][:, : c1 - c0],
                 lhsT=weights[which][:].bitcast(FP8X4),
-                lhsT_scale=w23_sc[:, which * N : (which + 1) * N],
+                lhsT_scale=(x_sc if which else w2_sc)[:, :N],
                 rhs=codes[:, c0:c1].bitcast(FP8X4),
                 rhs_scale=scales[:, c0:c1],
                 start=first,

from contextlib import ExitStack

import concourse.mybir as mybir

K, T, H, N = 512, 1024, 512, 128
FLOPS = 2 * K * H * T + 2 * 2 * H * N * T

F32 = mybir.dt.float32
BF16 = mybir.dt.bfloat16
I32 = mybir.dt.int32
U32 = mybir.dt.uint32
U16 = mybir.dt.uint16
U8 = mybir.dt.uint8
FP8X4 = mybir.dt.float8_e4m3fn_x4
ACT = mybir.ActivationFunctionType
ALU = mybir.AluOpType

P = 128
PACK = 4
HALF = 512
QUARTER = 256
EIGHTH = 128
SPLIT = 512


def tile_picked_wsagecat_maxrelu_l_kernel(
    tc, x_words, x_scales, w1, w2_words, w2_scales, w3_words, w3_scales, pos1, pos2, out
):
    nc = tc.nc
    with ExitStack() as ctx:
        keep = ctx.enter_context(tc.tile_pool(name="keep", bufs=1))
        psum = ctx.enter_context(tc.psum_pool(name="psum", bufs=1))

        def load_scales(tile, cols, src):
            for q in range(4):
                nc.sync.dma_start(
                    out=tile[32 * q : 32 * q + 4, cols].bitcast(I32),
                    in_=src[0, 4 * q : 4 * q + 4, :].bitcast(I32),
                )

        def load_words(tile, src):
            nc.sync.dma_start(out=tile.bitcast(I32), in_=src[0].rearrange("p n t -> p (n t)").bitcast(I32))

        x_sc = keep.tile([P, QUARTER], U8, name="x_sc", align_bytes=64)
        nc.vector.memset(x_sc[:].bitcast(U32), 0)
        w1_rows = w1.rearrange("(p j) c -> p j c", j=PACK)
        w1_parts = []
        for n, (c0, c1) in enumerate(((0, 256), (256, 384), (384, 512))):
            part = keep.tile([P, PACK, c1 - c0], F32, name=f"w1_raw{n}", tag=f"w1_raw{n}", align_bytes=64)
            nc.sync.dma_start(out=part[:], in_=w1_rows[:, :, c0:c1])
            w1_parts.append((slice(c0 // PACK, c1 // PACK), part[:].rearrange("p j (m t) -> p m t j", t=PACK)))
        for q in range(4):
            nc.sync.dma_start(
                out=x_sc[32 * q : 32 * q + 16, :].bitcast(I32),
                in_=x_scales[0, 4 * q : 4 * q + 4, :].bitcast(I32).rearrange("r (a c) -> a r c", a=4),
            )
        x_w = keep.tile([P, T], U32, name="x_w", tag="x_w", align_bytes=64)
        x_src = x_words[0].rearrange("p n t -> p (n t)").bitcast(I32)
        for c0 in (0, HALF):
            nc.sync.dma_start(out=x_w[:, c0 : c0 + HALF].bitcast(I32), in_=x_src[:, c0 : c0 + HALF])
        lists = []
        for name, src in (("pos1_sb", pos1), ("pos2_sb", pos2)):
            tile = keep.tile([P, T // 16], U16, name=name)
            nc.sync.dma_start(tile[:], src)
            lists.append(tile)

        w1_b = keep.tile([P, PACK, P, PACK], BF16, name="w1_b", tag="w1_b", align_bytes=64)
        w1_q = keep.tile([P, H], U32, name="w1_q", align_bytes=64)
        w1_sc = keep.tile([P, H], U8, name="w1_sc", align_bytes=64)
        w1_dst = w1_b[:].rearrange("p t m j -> p m t j")

        def quant_w1(c0, c1):
            nc.vector.quantize_mx(
                out=w1_q[:, c0:c1].bitcast(FP8X4),
                scales=w1_sc[:, c0:c1],
                in_=w1_b[:].rearrange("p t m j -> p (t m j)")[:, PACK * c0 : PACK * c1],
            )

        for rows, part in w1_parts[:2]:
            nc.vector.tensor_copy(out=w1_dst[:, rows, :, :], in_=part)
        quant_w1(3 * P, 3 * P + P // 2)
        rows, part = w1_parts[2]
        nc.vector.tensor_copy(out=w1_dst[:, rows, 3, :], in_=part[:, :, 3, :])
        nc.vector.tensor_copy(out=w1_dst[:, rows, 0, :], in_=part[:, :, 0, :])
        nc.scalar.activation(out=w1_dst[:, rows, 1:3, :], in_=part[:, :, 1:3, :], func=ACT.Copy)
        quant_w1(3 * P + P // 2, H)
        quant_w1(P, 3 * P)
        quant_w1(0, P)

        h = keep.tile([P, PACK * T], F32, name="h", align_bytes=64)
        copies = {t: keep.tile([P, T], F32, name=f"plane{t}", align_bytes=64) for t in (1, 2, 3)}

        def plane(t):
            return h[:, t * T : (t + 1) * T]

        filled = []

        def first_layer(t, c0, width, on_vector):
            acc = psum.tile([P, HALF], F32, name="h_acc", tag=f"bank{len(filled) % 4}")
            filled.append(acc)
            for a in range(c0 // QUARTER, (c0 + width) // QUARTER):
                cols = slice(a * QUARTER, (a + 1) * QUARTER)
                nc.tensor.matmul_mx(
                    out=acc[:, a * QUARTER - c0 : (a + 1) * QUARTER - c0],
                    lhsT=w1_q[:, t * P : (t + 1) * P].bitcast(FP8X4),
                    lhsT_scale=w1_sc[:, t * P : (t + 1) * P],
                    rhs=x_w[:, cols].bitcast(FP8X4),
                    rhs_scale=x_sc[4 * a :, :],
                    start=True,
                    stop=True,
                )
            dst = plane(t)[:, c0 : c0 + width]
            if on_vector:
                nc.vector.tensor_scalar_max(out=dst, in0=acc[:, :width], scalar1=0.0)
            else:
                nc.scalar.activation(out=dst, in_=acc[:, :width], func=ACT.Relu)

        def copy_half(t, c0):
            nc.sync.dma_start(out=copies[t][:, c0 : c0 + HALF], in_=plane(t)[:, c0 : c0 + HALF])

        for c0 in range(0, T, QUARTER):
            first_layer(3, c0, QUARTER, c0 % HALF == 0)
            if c0 % HALF:
                copy_half(3, c0 - QUARTER)
        for c0, c1 in ((0, QUARTER), (QUARTER, HALF), (HALF, T)):
            for t in (2, 1, 0):
                first_layer(t, c0, c1 - c0, (t, c0) == (2, 0))
                if t and c1 % HALF == 0:
                    copy_half(t, c1 - HALF)

        w3_w = keep.tile([P, N], U32, name="w3_w", tag="w1_raw0", align_bytes=64)
        w2_sc = keep.tile([P, N], U8, name="w2_sc", tag="w1_b", align_bytes=64)
        nc.gpsimd.memset(w2_sc[:].bitcast(U32), 0)
        load_words(w3_w[:], w3_words)
        load_scales(w2_sc, slice(0, N), w2_scales)
        load_scales(x_sc, slice(0, N), w3_scales)

        room = keep.tile([P, 10752], BF16, name="room", align_bytes=64)

        def bytes_at(start, count):
            return room[:, start : start + count]

        def woven(view):
            return view.rearrange("p (c t) -> p c t", t=PACK)

        def by_plane(view):
            return view.rearrange("p (t c) -> p t c", t=PACK)

        lead = 3584
        h_b = woven(bytes_at(lead, PACK * T))

        def weave_gpsimd(dst, src):
            nc.gpsimd.tensor_scalar(out=dst, in0=src, scalar1=1.0, scalar2=0.0, op0=ALU.mult, op1=ALU.add)

        for c0, c1 in ((0, QUARTER), (QUARTER, HALF - 4), (HALF - 4, T)):
            weave_gpsimd(h_b[:, c0:c1, :], h[:].rearrange("p (t c) -> p c t", t=PACK)[:, c0:c1, :])

        def offsets(d, c0, c1):
            return lists[d][:, c0 // 16 : c1 // 16]

        wide = T - SPLIT
        low_at = (8704, 5760)
        high_at = (9728, 7680)

        def gather_vector(d, t):
            start = high_at[d] if t >= 2 else low_at[d]
            nc.vector.tensor_copy(
                out=bytes_at(start, 2 * wide).rearrange("p (c e) -> p c e", e=2)[:, :, t % 2],
                in_=plane(t).indirect(offsets(d, SPLIT, T)),
            )

        def gather_scalar(dst, order, c0, c1):
            for t in order:
                for d in range(2):
                    nc.scalar.activation(
                        out=dst[:, d, t, :], in_=copies.get(t, h)[:].indirect(offsets(d, c0, c1)), func=ACT.Copy
                    )

        for d, t in ((0, 3), (1, 3), (0, 2), (1, 2), (0, 1), (0, 0)):
            gather_vector(d, t)
        got_a = keep.tile([P, 2, PACK, QUARTER], BF16, name="got_a", tag="x_w", align_bytes=64)
        gather_scalar(got_a, (3, 0, 2, 1), 0, QUARTER)

        h_q = keep.tile([P, T], U32, name="h_q", align_bytes=64)
        h_sc = keep.tile([P, T], U8, name="h_sc", align_bytes=64)
        z_q = keep.tile([P, T], U32, name="z_q", align_bytes=64)
        z_sc = keep.tile([P, T], U8, name="z_sc", align_bytes=64)
        res = keep.tile([P, T], F32, name="res", align_bytes=64)

        def quantize(codes, scales, values, c0, c1):
            nc.vector.quantize_mx(
                out=codes[:, c0:c1].bitcast(FP8X4),
                scales=scales[:, c0:c1],
                in_=values.rearrange("p c t -> p (c t)"),
            )

        accs = {}
        weights = {1: w3_w}

        def second_layer(c0, c1, which):
            first = c0 not in accs
            if first:
                accs[c0] = psum.tile([P, HALF], F32, name="out_acc", tag=f"bank{(4 + len(accs)) % 8}")
            codes, scales = (z_q, z_sc) if which else (h_q, h_sc)
            nc.tensor.matmul_mx(
                out=accs[c0][:, : c1 - c0],
                lhsT=weights[which][:].bitcast(FP8X4),
                lhsT_scale=(x_sc if which else w2_sc)[:, :N],
                rhs=codes[:, c0:c1].bitcast(FP8X4),
                rhs_scale=scales[:, c0:c1],
                start=first,
                stop=not first,
            )

        span_a, span_c, span_d = (0, 256), (256, 384), (384, 512)
        span_e, span_f = (512, 768), (768, 1024)

        for c0 in (0, HALF):
            quantize(h_q, h_sc, h_b[:, c0 : c0 + HALF, :], c0, c0 + HALF)

        rest = SPLIT - QUARTER
        got_d = bytes_at(lead + EIGHTH, 2 * PACK * rest).rearrange("p (d t c) -> p d t c", d=2, c=rest)
        gather_scalar(got_d, (3, 2, 1, 0), QUARTER, SPLIT)

        def largest(dst, first, second):
            nc.vector.tensor_tensor(out=dst, in0=first, in1=second, op=ALU.max)

        def store(c0, c1, on_vector):
            if on_vector:
                nc.vector.tensor_scalar_max(out=res[:, c0:c1], in0=accs[c0][:, : c1 - c0], scalar1=0.0)
            else:
                nc.scalar.activation(out=res[:, c0:c1], in_=accs[c0][:, : c1 - c0], func=ACT.Relu)
            nc.sync.dma_start(out=out[:, c0:c1], in_=res[:, c0:c1])

        def neighbours(values, c0, c1):
            quantize(z_q, z_sc, values, c0, c1)
            second_layer(c0, c1, 1)

        top_a = by_plane(bytes_at(1920, PACK * HALF))[:, :, :QUARTER]
        largest(top_a, got_a[:, 0], got_a[:, 1])
        weights[0] = keep.tile([P, N], U32, name="w2_w", tag="x_w", align_bytes=64)
        load_words(weights[0][:], w2_words)
        for span in (span_a, span_e, span_f, span_c, span_d):
            second_layer(*span, 0)
        z_a = keep.tile([P, QUARTER, PACK], BF16, name="z_a", align_bytes=64)
        weave_gpsimd(z_a[:], top_a.rearrange("p t c -> p c t"))
        for t in (1, 0):
            gather_vector(1, t)
        neighbours(z_a[:], *span_a)
        z_high = woven(bytes_at(0, PACK * HALF))
        z_d = keep.tile([P, QUARTER, PACK], BF16, name="z_d", align_bytes=64)

        def z_cols(c0, c1):
            return z_high[:, c0 - HALF : c1 - HALF, :] if c0 >= HALF else z_d[:, c0 - QUARTER : c1 - QUARTER, :]

        both = []
        for d in range(2):
            step = high_at[d] - low_at[d]
            halves = bytes_at(low_at[d], 2 * step).rearrange("p (u x) -> p u x", u=2)[:, :, : 2 * wide]
            both.append(halves.rearrange("p u (c e) -> p c u e", e=2))
        largest(z_cols(SPLIT, T).rearrange("p c (u e) -> p c u e", e=2), *both)
        top_d = by_plane(bytes_at(PACK * HALF, PACK * rest))
        largest(top_d[:, 1:], got_d[:, 0, 1:], got_d[:, 1, 1:])
        neighbours(z_cols(*span_e), *span_e)
        largest(top_d[:, 0], got_d[:, 0, 0], got_d[:, 1, 0])
        store(*span_a, False)
        neighbours(z_cols(*span_f), *span_f)
        for copy, c0, c1 in ((nc.scalar.copy, *span_c), (nc.vector.tensor_copy, *span_d)):
            copy(
                out=z_cols(c0, c1).rearrange("p (c i) t -> p c t i", i=4),
                in_=top_d[:, :, c0 - QUARTER : c1 - QUARTER].rearrange("p t (c i) -> p c t i", i=4),
            )
        for span in (span_d, span_c):
            neighbours(z_cols(*span), *span)
        for span, on_vector in ((span_e, False), (span_f, False), (span_d, True), (span_c, True)):
            store(*span, on_vector)
